import numpy as np
import ml_dtypes


def mxq(x, axis, fmt="e4m3"):
    dtype, down = {"e4m3": (ml_dtypes.float8_e4m3fn, 7), "e5m2": (ml_dtypes.float8_e5m2, 14)}[fmt]
    v = np.moveaxis(np.asarray(x, np.float32).astype(ml_dtypes.bfloat16).astype(np.float64), axis, -1)
    blocks = v.reshape(v.shape[:-1] + (-1, 32))
    amax = np.abs(blocks).max(-1, keepdims=True)
    byte = np.maximum(np.where(amax > 0, np.frexp(amax)[1] - 1 + 127, 0) - down, 1)
    scale = np.exp2(byte - 127.0)
    codes = (blocks / scale).astype(np.float32).astype(dtype).astype(np.float64)
    return np.moveaxis((codes * scale).reshape(v.shape), -1, axis)


WIDE = False


def mx_kscale(k):
    if not WIDE:
        return np.ones(k)
    levels = np.array([10, -10, 5, -5, 0])
    if k % 512:
        return np.exp2(np.random.permutation(np.resize(levels, k // 32))).repeat(32)
    a = np.empty((k // 512, 16))
    for p in range(k // 512):
        a[p, :8] = np.random.permutation(np.resize(levels, 8))
        for g in range(8):
            far = levels[np.abs(levels - a[p, g]) >= 10]
            a[p, g + 8] = far[np.random.randint(len(far))]
    return np.exp2(a.ravel()).repeat(32)


def f64(x):
    return np.asarray(x).astype(np.float64)


def striped(idx):
    return np.tile(idx.reshape(-1, 16).T, (8, 1)).astype(np.uint16)


def unstriped(offs):
    return offs[:16].T.reshape(-1).astype(np.int64)


E2M1 = np.array([0.0, 0.5, 1.0, 1.5, 2.0, 3.0, 4.0, 6.0, -0.0, -0.5, -1.0, -1.5, -2.0, -3.0, -4.0, -6.0])


def pack_weight(w, fmt):
    k, n = w.shape
    w = f64(np.asarray(w, np.float32).astype(ml_dtypes.bfloat16)).reshape(k // 32, 32, n)
    amax = np.abs(w).max(1)
    if fmt == "e4m3":
        byte = np.frexp(amax)[1] - 1 + 127 - 7
    else:
        mant, ex = np.frexp(amax / 6.0)
        byte = np.where(mant > 0.5, ex, ex - 1) + 127
    byte = np.clip(np.where(amax > 0, byte, 1), 1, 254)
    scaled = (w * np.exp2(127.0 - byte)[:, None, :]).reshape(k, n).astype(np.float32)
    by_word = np.ascontiguousarray(scaled.reshape(k // 512, 128, 4, n).transpose(0, 1, 3, 2))
    if fmt == "e4m3":
        words = by_word.astype(ml_dtypes.float8_e4m3fn).view(np.uint8)
    else:
        c = by_word.astype(ml_dtypes.float4_e2m1fn).view(np.uint8) & 0xF
        words = (c[..., 0::2] | (c[..., 1::2] << 4)).reshape(k // 512, 128, 2 * n)
    return np.ascontiguousarray(words), np.ascontiguousarray(byte.astype(np.uint8).reshape(k // 512, 16, n))


def unpack_weight(words, scales, fmt):
    g, _, n = scales.shape
    words = np.ascontiguousarray(words).reshape(g, 128, n, -1)
    if fmt == "e4m3":
        vals = words.view(ml_dtypes.float8_e4m3fn).astype(np.float64)
    else:
        nib = np.empty((g, 128, n, 4), np.uint8)
        nib[..., 0::2] = words & 0xF
        nib[..., 1::2] = words >> 4
        vals = E2M1[nib]
    vals = vals * np.repeat(np.exp2(scales.astype(np.float64) - 127.0), 8, axis=1)[..., None]
    return vals.transpose(0, 1, 3, 2).reshape(g * 512, n)


def gelu(v):
    return 0.5 * v * (1.0 + np.tanh(np.sqrt(2.0 / np.pi) * (v + 0.044715 * v**3)))


K, T, E, C, N = 512, 4096, 8, 256, 256
R = 2


def by_expert(wq, xq):
    return np.concatenate([wq[e].T @ xq[:, e * C:(e + 1) * C] for e in range(E)], axis=1)


def setup_inputs():
    n = np.random.standard_normal
    s = mx_kscale(K)[:, None]
    slot_token = np.concatenate([r * (T // R) + np.random.permutation(T // R)[:C // R] for e in range(E) for r in range(R)])
    w = [pack_weight(m, "e2m1") for m in n((E, K, N)) / np.sqrt(K) / s[None]]
    return {
        "xT": (n((K, T)) * s).astype(np.float32),
        "w_words": np.stack([m[0] for m in w]),
        "w_scales": np.stack([m[1] for m in w]),
        "b": (0.3 * n((N, E))).astype(np.float32),
        "offs": striped(slot_token),
    }


def reference(xT, w_words, w_scales, b, offs):
    idx = unstriped(offs)
    w = np.stack([unpack_weight(w_words[e], w_scales[e], "e2m1") for e in range(E)])
    xq = mxq(f64(xT)[:, idx], 0, "e4m3")
    y = by_expert(w, xq)
    y = gelu(y + np.repeat(f64(b), C, axis=1))
    return y.reshape(N, E, R, C // R).transpose(0, 2, 1, 3).reshape(N, E * C)

@@ -1,0 +1,135 @@
+from contextlib import ExitStack
+
+import concourse.mybir as mybir
+
+K, T, E, C, N = 512, 4096, 8, 256, 256
+R = 2
+P = 128
+PACK = 4
+S = E * C
+U = C // R
+FLOPS = 2 * K * N * S
+
+F32 = mybir.dt.float32
+BF16 = mybir.dt.bfloat16
+U32 = mybir.dt.uint32
+I32 = mybir.dt.int32
+U16 = mybir.dt.uint16
+U8 = mybir.dt.uint8
+FP8X4 = mybir.dt.float8_e4m3fn_x4
+FP4X4 = mybir.dt.float4_e2m1fn_x4
+ACT = mybir.ActivationFunctionType
+
+LOADS = (
+    ((0, 1024, 640), (1024, 1024, 640), (2048, 1024, 640), (3072, 1024, 640)),
+    ((0, 1024, 0), (1024, 1024, 0), (2048, 1024, 512), (3072, 512, 256), (3584, 512, 320)),
+)
+PIECE = 512
+GROUP = 16
+
+
+def tile_moe_eps_lin_gelu_kernel(tc, xT, w_words, w_scales, b, offs, out):
+    nc = tc.nc
+    with ExitStack() as ctx:
+        keep = ctx.enter_context(tc.tile_pool(name="keep", bufs=1))
+        psum = ctx.enter_context(tc.psum_pool(name="psum", bufs=1))
+
+        offsets = keep.tile([P, S // GROUP], U16, name="offsets")
+        w_sb = keep.tile([P, E, 2 * N], U8, name="w_sb", align_bytes=256)
+        ws_sb = keep.tile([P, E * N], U8, name="ws_sb", align_bytes=256)
+        bias = keep.tile([P, 2, E], F32, name="bias")
+        warm = keep.tile([P, 1], F32, name="warm")
+
+        x_rows = xT.rearrange("(p j) t -> p j t", j=PACK)
+        raws = []
+        for u in range(2):
+            for t0, w, v in LOADS[u]:
+                raw = keep.tile([P, 2, w], F32, name="raw%d_%d" % (u, t0))
+                nc.sync.dma_start(out=raw[:], in_=x_rows[:, 2 * u : 2 * u + 2, t0 : t0 + w])
+                raws.append(raw)
+                if u == 0 and t0 == 0:
+                    nc.sync.dma_start(offsets[:], offs)
+        nc.sync.dma_start(
+            out=w_sb[:].bitcast(I32), in_=w_words.rearrange("e a p c -> p (e a) c").bitcast(I32)
+        )
+        nc.vector.memset(warm[:], 0.0)
+        nc.scalar.activation(warm[:], warm[:], ACT.Gelu_apprx_tanh)
+        nc.vector.memset(ws_sb[:].bitcast(I32), 0)
+        for q in range(4):
+            nc.scalar.dma_start(
+                out=ws_sb[32 * q : 32 * q + 4, :].rearrange("q (e n) -> q e n", e=E).bitcast(I32),
+                in_=w_scales[:, 0, 4 * q : 4 * q + 4, :].rearrange("e q n -> q e n").bitcast(I32),
+            )
+        nc.scalar.dma_start(out=bias[:], in_=b.rearrange("(h p) e -> p h e", h=2))
+
+        tables = []
+        pieces = []
+        for u in range(2):
+            table = keep.tile([P, T, 2], BF16, name="table%d" % u, align_bytes=256)
+            tables.append(table)
+            for i, (t0, w, v) in enumerate(LOADS[u]):
+                raw = raws[len(LOADS[0]) * u + i]
+                dst = table[:, t0 : t0 + w, :].rearrange("p (c i) j -> p c j i", i=4)
+                src = raw[:].rearrange("p j (c i) -> p c j i", i=4)
+                if v > 0:
+                    nc.vector.tensor_copy(out=dst[:, : v // 4], in_=src[:, : v // 4])
+                if v < w:
+                    nc.scalar.activation(dst[:, v // 4 :], src[:, v // 4 :], ACT.Copy)
+            if u == 0:
+                words = table[:].rearrange("p t j -> p (t j)").bitcast(U32)
+                for g in range(S // PIECE):
+                    x4 = keep.tile([P, PIECE, PACK], BF16, name="x4_%d" % g, align_bytes=256)
+                    pieces.append(x4)
+                    lo = g * PIECE // GROUP
+                    hi = lo + PIECE // GROUP
+                    dst = x4[:].rearrange("p n j -> p (n j)").bitcast(U32).rearrange("p (n u) -> p n u", u=2)
+                    nc.vector.tensor_copy(dst[:, :, 0], words.indirect(offsets[:, lo:hi]))
+
+        result = keep.tile([P, 2, R, S // R], F32, name="result")
+        out_rows = out.rearrange("(h p) (m c) -> p h m c", h=2, m=R)
+        words = tables[1][:].rearrange("p t j -> p (t j)").bitcast(U32)
+
+        def gather(g):
+            lo = g * PIECE // GROUP
+            hi = lo + PIECE // GROUP
+            dst = pieces[g][:].rearrange("p n j -> p (n j)").bitcast(U32).rearrange("p (n u) -> p n u", u=2)
+            nc.vector.tensor_copy(dst[:, :, 1], words.indirect(offsets[:, lo:hi]))
+
+        def finish(g):
+            codes = keep.tile([P, PIECE], U32, name="codes%d" % g, align_bytes=256)
+            scales = keep.tile([P, PIECE], U8, name="scales%d" % g, align_bytes=256)
+            nc.vector.quantize_mx(
+                out=codes[:].bitcast(FP8X4), scales=scales[:], in_=pieces[g][:].rearrange("p n j -> p (n j)")
+            )
+            banks = []
+            for k in range(2):
+                e = 2 * g + k
+                bank = psum.tile([P, 2, C], F32, name="bank%d" % e)
+                banks.append(bank)
+                for h in range(2):
+                    nc.tensor.matmul_mx(
+                        out=bank[:, h, :],
+                        lhsT=w_sb[:, e, 256 * h : 256 * h + 256].bitcast(FP4X4),
+                        lhsT_scale=ws_sb[:, e * N + 128 * h : e * N + 128 * h + 128],
+                        rhs=codes[:, k * C : (k + 1) * C].bitcast(FP8X4),
+                        rhs_scale=scales[:, k * C : (k + 1) * C],
+                        start=True,
+                        stop=True,
+                    )
+            for h in range(2):
+                for k in range(2):
+                    e = 2 * g + k
+                    nc.scalar.activation(
+                        result[:, h, :, e * U : (e + 1) * U],
+                        banks[k][:, h, :].rearrange("p (m u) -> p m u", m=R),
+                        ACT.Gelu_apprx_tanh,
+                        bias=bias[:, h, e : e + 1],
+                    )
+                c0 = 2 * g * U
+                nc.sync.dma_start(out=out_rows[:, h, :, c0 : c0 + 2 * U], in_=result[:, h, :, c0 : c0 + 2 * U])
+
+        for g in range(S // PIECE):
+            gather(g)
+            if g > 0:
+                finish(g - 1)
+        finish(S // PIECE - 1)

@@ -62,8 +62,18 @@ def tile_moe_eps_lin_gelu_kernel(tc, xT, w_words, w_scales, b, offs, out):
             )
         nc.scalar.dma_start(out=bias[:], in_=b.rearrange("(h p) e -> p h e", h=2))
 
+        held_a = keep.tile([P, 2, PIECE], U32, name="held_a", align_bytes=256)
+        held_b = keep.tile([P, 3, PIECE], U32, name="held_b", align_bytes=256)
+        held_c = keep.tile([P, 2, PIECE], U32, name="held_c", align_bytes=256)
+        pairs = ((held_a, 0, 1), (held_b, 0, 2), (held_c, 0, 1), (held_b, 1, 2))
+
+        def gather(u, g):
+            lo = g * PIECE // GROUP
+            hi = lo + PIECE // GROUP
+            words = tables[u][:].rearrange("p t j -> p (t j)").bitcast(U32)
+            nc.vector.tensor_copy(pairs[g][0][:, pairs[g][1 + u], :], words.indirect(offsets[:, lo:hi]))
+
         tables = []
-        pieces = []
         for u in range(2):
             table = keep.tile([P, T, 2], BF16, name="table%d" % u, align_bytes=256)
             tables.append(table)
@@ -76,39 +86,41 @@ def tile_moe_eps_lin_gelu_kernel(tc, xT, w_words, w_scales, b, offs, out):
                 if v < w:
                     nc.scalar.activation(dst[:, v // 4 :], src[:, v // 4 :], ACT.Copy)
             if u == 0:
-                words = table[:].rearrange("p t j -> p (t j)").bitcast(U32)
                 for g in range(S // PIECE):
-                    x4 = keep.tile([P, PIECE, PACK], BF16, name="x4_%d" % g, align_bytes=256)
-                    pieces.append(x4)
-                    lo = g * PIECE // GROUP
-                    hi = lo + PIECE // GROUP
-                    dst = x4[:].rearrange("p n j -> p (n j)").bitcast(U32).rearrange("p (n u) -> p n u", u=2)
-                    nc.vector.tensor_copy(dst[:, :, 0], words.indirect(offsets[:, lo:hi]))
+                    gather(0, g)
 
         result = keep.tile([P, 2, R, S // R], F32, name="result")
         out_rows = out.rearrange("(h p) (m c) -> p h m c", h=2, m=R)
-        words = tables[1][:].rearrange("p t j -> p (t j)").bitcast(U32)
+        woven = [keep.tile([P, PIECE * PACK], BF16, name="woven%d" % g, align_bytes=256) for g in range(3)]
 
-        def gather(g):
-            lo = g * PIECE // GROUP
-            hi = lo + PIECE // GROUP
-            dst = pieces[g][:].rearrange("p n j -> p (n j)").bitcast(U32).rearrange("p (n u) -> p n u", u=2)
-            nc.vector.tensor_copy(dst[:, :, 1], words.indirect(offsets[:, lo:hi]))
+        def weave(g, lo, n, on_vector):
+            held, first, second = pairs[g]
+            src = held[:, first : second + 1 : second - first, lo : lo + n].rearrange("p u n -> p n u")
+            dst = woven[min(g, 2)][:, PACK * lo : PACK * (lo + n)]
+            if on_vector:
+                nc.vector.tensor_copy(
+                    out=dst.bitcast(I32).rearrange("p (n u) -> p n u", u=2), in_=src.bitcast(I32)
+                )
+            else:
+                nc.scalar.copy(dst.bitcast(U32).rearrange("p (n u) -> p n u", u=2), src)
 
-        def finish(g):
-            codes = keep.tile([P, PIECE], U32, name="codes%d" % g, align_bytes=256)
-            scales = keep.tile([P, PIECE], U8, name="scales%d" % g, align_bytes=256)
+        banks = {}
+
+        def multiply(g, lo, n):
+            codes = keep.tile([P, n], U32, name="codes%d_%d" % (g, lo), align_bytes=256)
+            scales = keep.tile([P, n], U8, name="scales%d_%d" % (g, lo), align_bytes=256)
             nc.vector.quantize_mx(
-                out=codes[:].bitcast(FP8X4), scales=scales[:], in_=pieces[g][:].rearrange("p n j -> p (n j)")
+                out=codes[:].bitcast(FP8X4),
+                scales=scales[:],
+                in_=woven[min(g, 2)][:, PACK * lo : PACK * (lo + n)],
             )
-            banks = []
-            for k in range(2):
-                e = 2 * g + k
-                bank = psum.tile([P, 2, C], F32, name="bank%d" % e)
-                banks.append(bank)
-                for h in range(2):
+            for h in range(2):
+                for k in range(n // C):
+                    e = (g * PIECE + lo) // C + k
+                    bank = psum.tile([P, C], F32, name="bank%d" % ((2 * e + h) % 8))
+                    banks[(e, h)] = bank
                     nc.tensor.matmul_mx(
-                        out=bank[:, h, :],
+                        out=bank[:],
                         lhsT=w_sb[:, e, 256 * h : 256 * h + 256].bitcast(FP4X4),
                         lhsT_scale=ws_sb[:, e * N + 128 * h : e * N + 128 * h + 128],
                         rhs=codes[:, k * C : (k + 1) * C].bitcast(FP8X4),
@@ -116,20 +128,32 @@ def tile_moe_eps_lin_gelu_kernel(tc, xT, w_words, w_scales, b, offs, out):
                         start=True,
                         stop=True,
                     )
+
+        def activate(g):
             for h in range(2):
                 for k in range(2):
                     e = 2 * g + k
                     nc.scalar.activation(
                         result[:, h, :, e * U : (e + 1) * U],
-                        banks[k][:, h, :].rearrange("p (m u) -> p m u", m=R),
+                        banks[(e, h)][:].rearrange("p (m u) -> p m u", m=R),
                         ACT.Gelu_apprx_tanh,
                         bias=bias[:, h, e : e + 1],
                     )
                 c0 = 2 * g * U
                 nc.sync.dma_start(out=out_rows[:, h, :, c0 : c0 + 2 * U], in_=result[:, h, :, c0 : c0 + 2 * U])
 
-        for g in range(S // PIECE):
-            gather(g)
-            if g > 0:
-                finish(g - 1)
-        finish(S // PIECE - 1)
+        for g in range(3):
+            gather(1, g)
+            weave(g, 0, PIECE, False)
+        multiply(0, 0, PIECE)
+        multiply(1, 0, PIECE)
+        activate(0)
+        gather(1, 3)
+        multiply(2, 0, PIECE)
+        activate(1)
+        weave(3, 0, C, True)
+        weave(3, C, C, True)
+        multiply(3, 0, C)
+        multiply(3, C, C)
+        activate(2)
+        activate(3)

@@ -21,8 +21,8 @@ FP4X4 = mybir.dt.float4_e2m1fn_x4
 ACT = mybir.ActivationFunctionType
 
 LOADS = (
-    ((0, 1024, 640), (1024, 1024, 640), (2048, 1024, 640), (3072, 1024, 640)),
-    ((0, 1024, 0), (1024, 1024, 0), (2048, 1024, 512), (3072, 512, 256), (3584, 512, 320)),
+    ((0, 2048, 1344), (2048, 2048, 1344)),
+    ((0, 2048, 768), (2048, 1024, 680), (3072, 512, 336), (3584, 512, 336)),
 )
 PIECE = 512
 GROUP = 16
@@ -56,11 +56,11 @@ def tile_moe_eps_lin_gelu_kernel(tc, xT, w_words, w_scales, b, offs, out):
         nc.scalar.activation(warm[:], warm[:], ACT.Gelu_apprx_tanh)
         nc.vector.memset(ws_sb[:].bitcast(I32), 0)
         for q in range(4):
-            nc.scalar.dma_start(
+            nc.sync.dma_start(
                 out=ws_sb[32 * q : 32 * q + 4, :].rearrange("q (e n) -> q e n", e=E).bitcast(I32),
                 in_=w_scales[:, 0, 4 * q : 4 * q + 4, :].rearrange("e q n -> q e n").bitcast(I32),
             )
-        nc.scalar.dma_start(out=bias[:], in_=b.rearrange("(h p) e -> p h e", h=2))
+        nc.sync.dma_start(out=bias[:], in_=b.rearrange("(h p) e -> p h e", h=2))
 
         held_a = keep.tile([P, 2, PIECE], U32, name="held_a", align_bytes=256)
         held_b = keep.tile([P, 3, PIECE], U32, name="held_b", align_bytes=256)

@@ -20,9 +20,9 @@ FP8X4 = mybir.dt.float8_e4m3fn_x4
 FP4X4 = mybir.dt.float4_e2m1fn_x4
 ACT = mybir.ActivationFunctionType
 
-LOADS = (
-    ((0, 2048, 1344), (2048, 2048, 1344)),
-    ((0, 2048, 768), (2048, 1024, 680), (3072, 512, 336), (3584, 512, 336)),
+STAGES = (
+    ((0, 4096, ((2048, 1344), (2048, 1344))),),
+    ((0, 2048, ((2048, 640),)), (2048, 2048, ((1024, 680), (512, 336), (512, 336)))),
 )
 PIECE = 512
 GROUP = 16
@@ -41,14 +41,23 @@ def tile_moe_eps_lin_gelu_kernel(tc, xT, w_words, w_scales, b, offs, out):
         warm = keep.tile([P, 1], F32, name="warm")
 
         x_rows = xT.rearrange("(p j) t -> p j t", j=PACK)
-        raws = []
+        casts = ([], [])
         for u in range(2):
-            for t0, w, v in LOADS[u]:
+            for t0, w, cuts in STAGES[u]:
                 raw = keep.tile([P, 2, w], F32, name="raw%d_%d" % (u, t0))
-                nc.sync.dma_start(out=raw[:], in_=x_rows[:, 2 * u : 2 * u + 2, t0 : t0 + w])
-                raws.append(raw)
-                if u == 0 and t0 == 0:
+                rows = x_rows[:, 2 * u : 2 * u + 2, t0 : t0 + w]
+                if len(cuts) == 1:
+                    nc.sync.dma_start(out=raw[:], in_=rows)
+                else:
+                    nc.sync.dma_start(out=raw[:, 0, :], in_=rows[:, 0, :])
+                if u == 0:
                     nc.sync.dma_start(offsets[:], offs)
+                c0 = 0
+                for n, v in cuts:
+                    if len(cuts) > 1:
+                        nc.sync.dma_start(out=raw[:, 1, c0 : c0 + n], in_=rows[:, 1, c0 : c0 + n])
+                    casts[u].append((t0 + c0, n, v, raw[:, :, c0 : c0 + n]))
+                    c0 = c0 + n
         nc.sync.dma_start(
             out=w_sb[:].bitcast(I32), in_=w_words.rearrange("e a p c -> p (e a) c").bitcast(I32)
         )
@@ -77,10 +86,9 @@ def tile_moe_eps_lin_gelu_kernel(tc, xT, w_words, w_scales, b, offs, out):
         for u in range(2):
             table = keep.tile([P, T, 2], BF16, name="table%d" % u, align_bytes=256)
             tables.append(table)
-            for i, (t0, w, v) in enumerate(LOADS[u]):
-                raw = raws[len(LOADS[0]) * u + i]
+            for t0, w, v, raw in casts[u]:
                 dst = table[:, t0 : t0 + w, :].rearrange("p (c i) j -> p c j i", i=4)
-                src = raw[:].rearrange("p j (c i) -> p c j i", i=4)
+                src = raw.rearrange("p j (c i) -> p c j i", i=4)
                 if v > 0:
                     nc.vector.tensor_copy(out=dst[:, : v // 4], in_=src[:, : v // 4])
                 if v < w:

@@ -20,9 +20,9 @@ FP8X4 = mybir.dt.float8_e4m3fn_x4
 FP4X4 = mybir.dt.float4_e2m1fn_x4
 ACT = mybir.ActivationFunctionType
 
-STAGES = (
-    ((0, 4096, ((2048, 1344), (2048, 1344))),),
-    ((0, 2048, ((2048, 640),)), (2048, 2048, ((1024, 680), (512, 336), (512, 336)))),
+CUTS = (
+    ((2432, 1616), (1664, 1104)),
+    ((1152, 704), (1024, 680), (832, 552), (640, 424), (448, 296)),
 )
 PIECE = 512
 GROUP = 16
@@ -40,24 +40,21 @@ def tile_moe_eps_lin_gelu_kernel(tc, xT, w_words, w_scales, b, offs, out):
         bias = keep.tile([P, 2, E], F32, name="bias")
         warm = keep.tile([P, 1], F32, name="warm")
 
-        x_rows = xT.rearrange("(p j) t -> p j t", j=PACK)
+        x_flat = xT.rearrange("(p j) t -> p (j t)", j=PACK)
+        raw = keep.tile([P, PACK * T], F32, name="raw")
+        raw_rows = raw[:].rearrange("p (j t) -> p j t", j=PACK)
         casts = ([], [])
+        begin = 0
         for u in range(2):
-            for t0, w, cuts in STAGES[u]:
-                raw = keep.tile([P, 2, w], F32, name="raw%d_%d" % (u, t0))
-                rows = x_rows[:, 2 * u : 2 * u + 2, t0 : t0 + w]
-                if len(cuts) == 1:
-                    nc.sync.dma_start(out=raw[:], in_=rows)
-                else:
-                    nc.sync.dma_start(out=raw[:, 0, :], in_=rows[:, 0, :])
-                if u == 0:
+            t0 = 0
+            for n, v in CUTS[u]:
+                end = (2 * u + 1) * T + t0 + n
+                nc.sync.dma_start(out=raw[:, begin:end], in_=x_flat[:, begin:end])
+                if begin == 0:
                     nc.sync.dma_start(offsets[:], offs)
-                c0 = 0
-                for n, v in cuts:
-                    if len(cuts) > 1:
-                        nc.sync.dma_start(out=raw[:, 1, c0 : c0 + n], in_=rows[:, 1, c0 : c0 + n])
-                    casts[u].append((t0 + c0, n, v, raw[:, :, c0 : c0 + n]))
-                    c0 = c0 + n
+                casts[u].append((t0, n, v, raw_rows[:, 2 * u : 2 * u + 2, t0 : t0 + n]))
+                begin = end
+                t0 = t0 + n
         nc.sync.dma_start(
             out=w_sb[:].bitcast(I32), in_=w_words.rearrange("e a p c -> p (e a) c").bitcast(I32)
         )
@@ -86,9 +83,9 @@ def tile_moe_eps_lin_gelu_kernel(tc, xT, w_words, w_scales, b, offs, out):
         for u in range(2):
             table = keep.tile([P, T, 2], BF16, name="table%d" % u, align_bytes=256)
             tables.append(table)
-            for t0, w, v, raw in casts[u]:
+            for t0, w, v, rows in casts[u]:
                 dst = table[:, t0 : t0 + w, :].rearrange("p (c i) j -> p c j i", i=4)
-                src = raw.rearrange("p j (c i) -> p c j i", i=4)
+                src = rows.rearrange("p j (c i) -> p c j i", i=4)
                 if v > 0:
                     nc.vector.tensor_copy(out=dst[:, : v // 4], in_=src[:, : v // 4])
                 if v < w:

@@ -103,8 +103,10 @@ def tile_moe_eps_lin_gelu_kernel(tc, xT, w_words, w_scales, b, offs, out):
             src = held[:, first : second + 1 : second - first, lo : lo + n].rearrange("p u n -> p n u")
             dst = woven[min(g, 2)][:, PACK * lo : PACK * (lo + n)]
             if on_vector:
+                halves = held[:, first : second + 1 : second - first, lo : lo + n].bitcast(BF16)
                 nc.vector.tensor_copy(
-                    out=dst.bitcast(I32).rearrange("p (n u) -> p n u", u=2), in_=src.bitcast(I32)
+                    out=dst.rearrange("p (c i u j) -> p c u i j", i=4, u=2, j=2),
+                    in_=halves.rearrange("p u (c i j) -> p c u i j", i=4, j=2),
                 )
             else:
                 nc.scalar.copy(dst.bitcast(U32).rearrange("p (n u) -> p n u", u=2), src)

@@ -21,7 +21,7 @@ FP4X4 = mybir.dt.float4_e2m1fn_x4
 ACT = mybir.ActivationFunctionType
 
 CUTS = (
-    ((2432, 1616), (1664, 1104)),
+    ((1920, 1280), (1280, 848), (896, 592)),
     ((1152, 704), (1024, 680), (832, 552), (640, 424), (448, 296)),
 )
 PIECE = 512
@@ -41,7 +41,7 @@ def tile_moe_eps_lin_gelu_kernel(tc, xT, w_words, w_scales, b, offs, out):
         warm = keep.tile([P, 1], F32, name="warm")
 
         x_flat = xT.rearrange("(p j) t -> p (j t)", j=PACK)
-        raw = keep.tile([P, PACK * T], F32, name="raw")
+        raw = keep.tile([P, PACK * T], F32, name="raw", align_bytes=512)
         raw_rows = raw[:].rearrange("p (j t) -> p j t", j=PACK)
         casts = ([], [])
         begin = 0
@@ -94,7 +94,7 @@ def tile_moe_eps_lin_gelu_kernel(tc, xT, w_words, w_scales, b, offs, out):
                 for g in range(S // PIECE):
                     gather(0, g)
 
-        result = keep.tile([P, 2, R, S // R], F32, name="result")
+        result = keep.tile([P, 2, R, S // R], F32, name="result", align_bytes=512)
         out_rows = out.rearrange("(h p) (m c) -> p h m c", h=2, m=R)
         woven = [keep.tile([P, PIECE * PACK], BF16, name="woven%d" % g, align_bytes=256) for g in range(3)]
 

@@ -98,11 +98,18 @@ def tile_moe_eps_lin_gelu_kernel(tc, xT, w_words, w_scales, b, offs, out):
         out_rows = out.rearrange("(h p) (m c) -> p h m c", h=2, m=R)
         woven = [keep.tile([P, PIECE * PACK], BF16, name="woven%d" % g, align_bytes=256) for g in range(3)]
 
+        def place(g, lo, n):
+            if (g, lo) == (2, C):
+                return woven[1][:, PACK * lo : PACK * (lo + n)]
+            return woven[min(g, 2)][:, PACK * lo : PACK * (lo + n)]
+
         def weave(g, lo, n, on_vector):
             held, first, second = pairs[g]
             src = held[:, first : second + 1 : second - first, lo : lo + n].rearrange("p u n -> p n u")
-            dst = woven[min(g, 2)][:, PACK * lo : PACK * (lo + n)]
-            if on_vector:
+            dst = place(g, lo, n)
+            if on_vector is None:
+                nc.gpsimd.tensor_copy(dst.bitcast(U32).rearrange("p (n u) -> p n u", u=2), src)
+            elif on_vector:
                 halves = held[:, first : second + 1 : second - first, lo : lo + n].bitcast(BF16)
                 nc.vector.tensor_copy(
                     out=dst.rearrange("p (c i u j) -> p c u i j", i=4, u=2, j=2),
@@ -119,7 +126,7 @@ def tile_moe_eps_lin_gelu_kernel(tc, xT, w_words, w_scales, b, offs, out):
             nc.vector.quantize_mx(
                 out=codes[:].bitcast(FP8X4),
                 scales=scales[:],
-                in_=woven[min(g, 2)][:, PACK * lo : PACK * (lo + n)],
+                in_=place(g, lo, n),
             )
             for h in range(2):
                 for k in range(n // C):
@@ -151,12 +158,15 @@ def tile_moe_eps_lin_gelu_kernel(tc, xT, w_words, w_scales, b, offs, out):
 
         for g in range(3):
             gather(1, g)
-            weave(g, 0, PIECE, False)
-        multiply(0, 0, PIECE)
+            weave(g, 0, PIECE if g < 2 else C, False)
+        multiply(0, 0, C)
+        multiply(0, C, C)
         multiply(1, 0, PIECE)
+        weave(2, C, C, None)
         activate(0)
+        multiply(2, 0, C)
         gather(1, 3)
-        multiply(2, 0, PIECE)
+        multiply(2, C, C)
         activate(1)
         weave(3, 0, C, True)
         weave(3, C, C, True)

@@ -22,7 +22,7 @@ ACT = mybir.ActivationFunctionType
 
 CUTS = (
     ((1920, 1280), (1280, 848), (896, 592)),
-    ((1152, 704), (1024, 680), (832, 552), (640, 424), (448, 296)),
+    ((1280, 856), (1024, 680), (768, 512), (640, 424), (384, 256)),
 )
 PIECE = 512
 GROUP = 16
@@ -35,13 +35,13 @@ def tile_moe_eps_lin_gelu_kernel(tc, xT, w_words, w_scales, b, offs, out):
         psum = ctx.enter_context(tc.psum_pool(name="psum", bufs=1))
 
         offsets = keep.tile([P, S // GROUP], U16, name="offsets")
-        w_sb = keep.tile([P, E, 2 * N], U8, name="w_sb", align_bytes=256)
+        w_sb = keep.tile([P, E, 2 * N], U8, name="w_sb", align_bytes=512)
         ws_sb = keep.tile([P, E * N], U8, name="ws_sb", align_bytes=256)
         bias = keep.tile([P, 2, E], F32, name="bias")
         warm = keep.tile([P, 1], F32, name="warm")
 
         x_flat = xT.rearrange("(p j) t -> p (j t)", j=PACK)
-        raw = keep.tile([P, PACK * T], F32, name="raw", align_bytes=512)
+        raw = keep.tile([P, PACK * T], F32, name="raw", align_bytes=1024)
         raw_rows = raw[:].rearrange("p (j t) -> p j t", j=PACK)
         casts = ([], [])
         begin = 0
@@ -94,7 +94,7 @@ def tile_moe_eps_lin_gelu_kernel(tc, xT, w_words, w_scales, b, offs, out):
                 for g in range(S // PIECE):
                     gather(0, g)
 
-        result = keep.tile([P, 2, R, S // R], F32, name="result", align_bytes=512)
+        result = keep.tile([P, 2, R, S // R], F32, name="result", align_bytes=1024)
         out_rows = out.rearrange("(h p) (m c) -> p h m c", h=2, m=R)
         woven = [keep.tile([P, PIECE * PACK], BF16, name="woven%d" % g, align_bytes=256) for g in range(3)]
 

@@ -8,6 +8,7 @@ P = 128
 PACK = 4
 S = E * C
 U = C // R
+HALF = T // R
 FLOPS = 2 * K * N * S
 
 F32 = mybir.dt.float32
@@ -20,12 +21,11 @@ FP8X4 = mybir.dt.float8_e4m3fn_x4
 FP4X4 = mybir.dt.float4_e2m1fn_x4
 ACT = mybir.ActivationFunctionType
 
-CUTS = (
-    ((1920, 1280), (1280, 848), (896, 592)),
-    ((1280, 856), (1024, 680), (768, 512), (640, 424), (384, 256)),
-)
-PIECE = 512
+EARLY_VECTOR = 1360
+FIRST_CUTS = ((1664, 1112), (1152, 768), (768, 512), (512, 344))
+LATE_CUTS = (768, 768, 512)
 GROUP = 16
+ROW = 3 * C
 
 
 def tile_moe_eps_lin_gelu_kernel(tc, xT, w_words, w_scales, b, offs, out):
@@ -40,24 +40,30 @@ def tile_moe_eps_lin_gelu_kernel(tc, xT, w_words, w_scales, b, offs, out):
         bias = keep.tile([P, 2, E], F32, name="bias")
         warm = keep.tile([P, 1], F32, name="warm")
 
+        x_rows = xT.rearrange("(p j) t -> p j t", j=PACK)
         x_flat = xT.rearrange("(p j) t -> p (j t)", j=PACK)
-        raw = keep.tile([P, PACK * T], F32, name="raw", align_bytes=1024)
-        raw_rows = raw[:].rearrange("p (j t) -> p j t", j=PACK)
-        casts = ([], [])
+
+        raw_early = keep.tile([P, 2, HALF], F32, name="raw_early", align_bytes=1024)
+        nc.sync.dma_start(out=raw_early[:], in_=x_rows[:, 2:4, 0:HALF])
+        nc.sync.dma_start(offsets[:], offs)
+        raw_first = keep.tile([P, 2 * T], F32, name="raw_first", align_bytes=1024)
         begin = 0
-        for u in range(2):
-            t0 = 0
-            for n, v in CUTS[u]:
-                end = (2 * u + 1) * T + t0 + n
-                nc.sync.dma_start(out=raw[:, begin:end], in_=x_flat[:, begin:end])
-                if begin == 0:
-                    nc.sync.dma_start(offsets[:], offs)
-                casts[u].append((t0, n, v, raw_rows[:, 2 * u : 2 * u + 2, t0 : t0 + n]))
-                begin = end
-                t0 = t0 + n
-        nc.sync.dma_start(
-            out=w_sb[:].bitcast(I32), in_=w_words.rearrange("e a p c -> p (e a) c").bitcast(I32)
-        )
+        t0 = 0
+        for n, v in FIRST_CUTS:
+            end = T + t0 + n
+            nc.sync.dma_start(out=raw_first[:, begin:end], in_=x_flat[:, begin:end])
+            begin = end
+            t0 = t0 + n
+        raw_late = []
+        t0 = HALF
+        for i, n in enumerate(LATE_CUTS):
+            skip = 5 * C if i == len(LATE_CUTS) - 1 else 0
+            room = keep.tile([P, skip + 2 * n], F32, name="raw_late%d" % i, align_bytes=1024)
+            rows = room[:, skip:].rearrange("p (j t) -> p j t", j=2)
+            nc.sync.dma_start(out=rows, in_=x_rows[:, 2:4, t0 : t0 + n])
+            raw_late.append((room, rows, t0, n))
+            t0 = t0 + n
+
         nc.vector.memset(warm[:], 0.0)
         nc.scalar.activation(warm[:], warm[:], ACT.Gelu_apprx_tanh)
         nc.vector.memset(ws_sb[:].bitcast(I32), 0)
@@ -66,111 +72,154 @@ def tile_moe_eps_lin_gelu_kernel(tc, xT, w_words, w_scales, b, offs, out):
                 out=ws_sb[32 * q : 32 * q + 4, :].rearrange("q (e n) -> q e n", e=E).bitcast(I32),
                 in_=w_scales[:, 0, 4 * q : 4 * q + 4, :].rearrange("e q n -> q e n").bitcast(I32),
             )
+        nc.sync.dma_start(
+            out=w_sb[:].bitcast(I32), in_=w_words.rearrange("e a p c -> p (e a) c").bitcast(I32)
+        )
         nc.sync.dma_start(out=bias[:], in_=b.rearrange("(h p) e -> p h e", h=2))
 
-        held_a = keep.tile([P, 2, PIECE], U32, name="held_a", align_bytes=256)
-        held_b = keep.tile([P, 3, PIECE], U32, name="held_b", align_bytes=256)
-        held_c = keep.tile([P, 2, PIECE], U32, name="held_c", align_bytes=256)
-        pairs = ((held_a, 0, 1), (held_b, 0, 2), (held_c, 0, 1), (held_b, 1, 2))
+        seconds = keep.tile([P, 3 * HALF, 2], BF16, name="seconds", align_bytes=256)
+        firsts = keep.tile([P, T, 2], BF16, name="firsts", align_bytes=256)
+        second_words = seconds[:].rearrange("p t j -> p (t j)").bitcast(U32)
+        first_words = firsts[:].rearrange("p t j -> p (t j)").bitcast(U32)
+        nc.vector.memset(seconds[:, HALF:T, :].rearrange("p t j -> p (t j)").bitcast(I32), 0)
 
-        def gather(u, g):
-            lo = g * PIECE // GROUP
-            hi = lo + PIECE // GROUP
-            words = tables[u][:].rearrange("p t j -> p (t j)").bitcast(U32)
-            nc.vector.tensor_copy(pairs[g][0][:, pairs[g][1 + u], :], words.indirect(offsets[:, lo:hi]))
+        def cast(table, rows, v):
+            n = rows.shape[2]
+            dst = table.rearrange("p (c i) j -> p c j i", i=4)
+            src = rows.rearrange("p j (c i) -> p c j i", i=4)
+            if v > 0:
+                nc.vector.tensor_copy(out=dst[:, : v // 4], in_=src[:, : v // 4])
+            if v < n:
+                nc.scalar.activation(dst[:, v // 4 :], src[:, v // 4 :], ACT.Copy)
 
-        tables = []
-        for u in range(2):
-            table = keep.tile([P, T, 2], BF16, name="table%d" % u, align_bytes=256)
-            tables.append(table)
-            for t0, w, v, rows in casts[u]:
-                dst = table[:, t0 : t0 + w, :].rearrange("p (c i) j -> p c j i", i=4)
-                src = rows.rearrange("p j (c i) -> p c j i", i=4)
-                if v > 0:
-                    nc.vector.tensor_copy(out=dst[:, : v // 4], in_=src[:, : v // 4])
-                if v < w:
-                    nc.scalar.activation(dst[:, v // 4 :], src[:, v // 4 :], ACT.Copy)
-            if u == 0:
-                for g in range(S // PIECE):
-                    gather(0, g)
+        held_a = keep.tile([P, 5, ROW], U32, name="held_a", align_bytes=256)
+        held_b = keep.tile([P, 2, ROW], U32, name="held_b", align_bytes=256)
+        small = (0, 2, held_a, 2, 3, 4)
+        mid = (2, 3, held_a, 0, 1, 4)
+        last = (5, 3, held_b, 0, 1, 1)
 
-        result = keep.tile([P, 2, R, S // R], F32, name="result", align_bytes=1024)
-        out_rows = out.rearrange("(h p) (m c) -> p h m c", h=2, m=R)
-        woven = [keep.tile([P, PIECE * PACK], BF16, name="woven%d" % g, align_bytes=256) for g in range(3)]
+        def gather(group, which):
+            e0, count, held = group[:3]
+            lo, hi = 0, count * C
+            if count == 3 and which == 1:
+                hi = hi - U
+            if count == 3 and which == 2:
+                lo = U
+            window = (first_words, second_words[:, :T], second_words[:, HALF:])[which]
+            entries = offsets[:, (e0 * C + lo) // GROUP : (e0 * C + hi) // GROUP]
+            nc.vector.tensor_copy(held[:, group[3 + which], lo:hi], window.indirect(entries))
 
-        def place(g, lo, n):
-            if (g, lo) == (2, C):
-                return woven[1][:, PACK * lo : PACK * (lo + n)]
-            return woven[min(g, 2)][:, PACK * lo : PACK * (lo + n)]
-
-        def weave(g, lo, n, on_vector):
-            held, first, second = pairs[g]
-            src = held[:, first : second + 1 : second - first, lo : lo + n].rearrange("p u n -> p n u")
-            dst = place(g, lo, n)
-            if on_vector is None:
-                nc.gpsimd.tensor_copy(dst.bitcast(U32).rearrange("p (n u) -> p n u", u=2), src)
-            elif on_vector:
-                halves = held[:, first : second + 1 : second - first, lo : lo + n].bitcast(BF16)
-                nc.vector.tensor_copy(
-                    out=dst.rearrange("p (c i u j) -> p c u i j", i=4, u=2, j=2),
-                    in_=halves.rearrange("p u (c i j) -> p c u i j", i=4, j=2),
-                )
+        def weave(group, rank, dst, engine):
+            count, held, first = group[1:4]
+            second = group[4 + rank]
+            src = held[:, first : second + 1 : second - first, : count * C]
+            src = src.rearrange("p u (e r n) -> p r e n u", r=R, n=U)[:, rank]
+            words = dst.bitcast(U32).rearrange("p (e n u) -> p e n u", n=U, u=2)
+            if engine == "gpsimd":
+                nc.gpsimd.tensor_copy(words, src)
+            elif engine == "scalar":
+                nc.scalar.copy(words, src)
             else:
-                nc.scalar.copy(dst.bitcast(U32).rearrange("p (n u) -> p n u", u=2), src)
+                nc.vector.tensor_copy(
+                    dst.bitcast(I32).rearrange("p (e n u) -> p e n u", n=U, u=2),
+                    held[:].bitcast(I32)[:, first : second + 1 : second - first, : count * C].rearrange(
+                        "p u (e r n) -> p r e n u", r=R, n=U
+                    )[:, rank],
+                )
 
-        banks = {}
+        sums = {}
+        turn = [0]
 
-        def multiply(g, lo, n):
-            codes = keep.tile([P, n], U32, name="codes%d_%d" % (g, lo), align_bytes=256)
-            scales = keep.tile([P, n], U8, name="scales%d_%d" % (g, lo), align_bytes=256)
-            nc.vector.quantize_mx(
-                out=codes[:].bitcast(FP8X4),
-                scales=scales[:],
-                in_=place(g, lo, n),
-            )
-            for h in range(2):
-                for k in range(n // C):
-                    e = (g * PIECE + lo) // C + k
-                    bank = psum.tile([P, C], F32, name="bank%d" % ((2 * e + h) % 8))
-                    banks[(e, h)] = bank
-                    nc.tensor.matmul_mx(
-                        out=bank[:],
-                        lhsT=w_sb[:, e, 256 * h : 256 * h + 256].bitcast(FP4X4),
-                        lhsT_scale=ws_sb[:, e * N + 128 * h : e * N + 128 * h + 128],
-                        rhs=codes[:, k * C : (k + 1) * C].bitcast(FP8X4),
-                        rhs_scale=scales[:, k * C : (k + 1) * C],
-                        start=True,
-                        stop=True,
-                    )
+        def multiply(values, blocks):
+            n = U * len(blocks)
+            name = "%d_%d" % blocks[0]
+            codes = keep.tile([P, n], U32, name="codes" + name, align_bytes=256)
+            scales = keep.tile([P, n], U8, name="scales" + name, align_bytes=256)
+            nc.vector.quantize_mx(out=codes[:].bitcast(FP8X4), scales=scales[:], in_=values)
+            for k0 in range(0, len(blocks), 2):
+                for h in range(2):
+                    bank = psum.tile([P, 2, U], F32, name="bank%d" % (turn[0] % 8))
+                    turn[0] = turn[0] + 1
+                    for k in range(k0, min(k0 + 2, len(blocks))):
+                        rank, e = blocks[k]
+                        sums[(rank, e, h)] = bank[:, k - k0, :]
+                        nc.tensor.matmul_mx(
+                            out=bank[:, k - k0, :],
+                            lhsT=w_sb[:, e, 256 * h : 256 * h + 256].bitcast(FP4X4),
+                            lhsT_scale=ws_sb[:, e * N + 128 * h : e * N + 128 * h + 128],
+                            rhs=codes[:, k * U : (k + 1) * U].bitcast(FP8X4),
+                            rhs_scale=scales[:, k * U : (k + 1) * U],
+                            start=True,
+                            stop=True,
+                        )
 
-        def activate(g):
-            for h in range(2):
-                for k in range(2):
-                    e = 2 * g + k
-                    nc.scalar.activation(
-                        result[:, h, :, e * U : (e + 1) * U],
-                        banks[(e, h)][:].rearrange("p (m u) -> p m u", m=R),
-                        ACT.Gelu_apprx_tanh,
-                        bias=bias[:, h, e : e + 1],
-                    )
-                c0 = 2 * g * U
-                nc.sync.dma_start(out=out_rows[:, h, :, c0 : c0 + 2 * U], in_=result[:, h, :, c0 : c0 + 2 * U])
+        out_rows = out.rearrange("(h p) c -> p h c", h=2)
+        results = {}
+        for rank, e0, count in ((0, 0, 4), (0, 4, 4), (1, 0, 2), (1, 2, 3), (1, 5, 3)):
+            result = keep.tile([P, 2, count * U], F32, name="result%d_%d" % (rank, e0), align_bytes=1024)
+            for k in range(count):
+                results[(rank, e0 + k)] = (result, k)
 
-        for g in range(3):
-            gather(1, g)
-            weave(g, 0, PIECE if g < 2 else C, False)
-        multiply(0, 0, C)
-        multiply(0, C, C)
-        multiply(1, 0, PIECE)
-        weave(2, C, C, None)
-        activate(0)
-        multiply(2, 0, C)
-        gather(1, 3)
-        multiply(2, C, C)
-        activate(1)
-        weave(3, 0, C, True)
-        weave(3, C, C, True)
-        multiply(3, 0, C)
-        multiply(3, C, C)
-        activate(2)
-        activate(3)
+        def activate(blocks):
+            for k0 in range(0, len(blocks), 2):
+                for h in range(2):
+                    for rank, e in blocks[k0 : k0 + 2]:
+                        result, k = results[(rank, e)]
+                        nc.scalar.activation(
+                            result[:, h, k * U : (k + 1) * U],
+                            sums[(rank, e, h)],
+                            ACT.Gelu_apprx_tanh,
+                            bias=bias[:, h, e : e + 1],
+                        )
+
+        def store(rank, e0, halves):
+            result = results[(rank, e0)][0]
+            c0 = rank * (S // R) + e0 * U
+            nc.sync.dma_start(out=out_rows[:, halves, c0 : c0 + result.shape[2]], in_=result[:, halves, :])
+
+        block = PACK * U
+        cast(seconds[:, :HALF, :], raw_early[:], EARLY_VECTOR)
+        for group in (small, mid, last):
+            gather(group, 1)
+        first_rows = raw_first[:].rearrange("p (j t) -> p j t", j=2)
+        t0 = 0
+        for n, v in FIRST_CUTS:
+            cast(firsts[:, t0 : t0 + n, :], first_rows[:, :, t0 : t0 + n], v)
+            t0 = t0 + n
+        woven = raw_late[-1][0][:].bitcast(BF16)
+        later = keep.tile([P, 3 * block], BF16, name="later", align_bytes=256)
+        gather(small, 0)
+        weave(small, 0, woven[:, : 2 * block], "gpsimd")
+        gather(mid, 0)
+        weave(mid, 0, woven[:, 2 * block : 5 * block], "gpsimd")
+        gather(last, 0)
+        for room, rows, t0, n in raw_late:
+            cast(seconds[:, HALF + t0 : HALF + t0 + n, :], rows, 0)
+        weave(last, 0, woven[:, 5 * block : 8 * block], "scalar")
+        multiply(woven[:, : 4 * block], [(0, 0), (0, 1), (0, 2), (0, 3)])
+        gather(mid, 2)
+        weave(mid, 1, later[:], "gpsimd")
+        multiply(woven[:, 4 * block : 8 * block], [(0, 4), (0, 5), (0, 6), (0, 7)])
+        gather(last, 2)
+        activate([(0, 0), (0, 1), (0, 2), (0, 3)])
+        store(0, 0, slice(0, 2))
+        activate([(0, 4), (0, 5), (0, 6), (0, 7)])
+        store(0, 4, slice(0, 2))
+        multiply(later[:, : 2 * block], [(1, 2), (1, 3)])
+        multiply(later[:, 2 * block :], [(1, 4)])
+        weave(last, 1, later[:], "gpsimd")
+        gather(small, 2)
+        activate([(1, 2), (1, 3)])
+        activate([(1, 4)])
+        store(1, 2, slice(0, 2))
+        multiply(later[:, : 2 * block], [(1, 5), (1, 6)])
+        final = held_b[:, 0, : 2 * C].bitcast(BF16)
+        weave(small, 1, final, "vector")
+        multiply(later[:, 2 * block :], [(1, 7)])
+        multiply(final, [(1, 0), (1, 1)])
+        activate([(1, 5), (1, 6)])
+        activate([(1, 7)])
+        store(1, 5, slice(0, 2))
+        activate([(1, 0), (1, 1)])
+        store(1, 0, slice(0, 1))
+        store(1, 0, slice(1, 2))

@@ -109,10 +109,10 @@ def tile_moe_eps_lin_gelu_kernel(tc, xT, w_words, w_scales, b, offs, out):
             entries = offsets[:, (e0 * C + lo) // GROUP : (e0 * C + hi) // GROUP]
             nc.vector.tensor_copy(held[:, group[3 + which], lo:hi], window.indirect(entries))
 
-        def weave(group, rank, dst, engine):
-            count, held, first = group[1:4]
+        def weave(group, rank, lo, hi, dst, engine):
+            held, first = group[2:4]
             second = group[4 + rank]
-            src = held[:, first : second + 1 : second - first, : count * C]
+            src = held[:, first : second + 1 : second - first, lo * C : hi * C]
             src = src.rearrange("p u (e r n) -> p r e n u", r=R, n=U)[:, rank]
             words = dst.bitcast(U32).rearrange("p (e n u) -> p e n u", n=U, u=2)
             if engine == "gpsimd":
@@ -122,7 +122,7 @@ def tile_moe_eps_lin_gelu_kernel(tc, xT, w_words, w_scales, b, offs, out):
             else:
                 nc.vector.tensor_copy(
                     dst.bitcast(I32).rearrange("p (e n u) -> p e n u", n=U, u=2),
-                    held[:].bitcast(I32)[:, first : second + 1 : second - first, : count * C].rearrange(
+                    held[:].bitcast(I32)[:, first : second + 1 : second - first, lo * C : hi * C].rearrange(
                         "p u (e r n) -> p r e n u", r=R, n=U
                     )[:, rank],
                 )
@@ -155,14 +155,14 @@ def tile_moe_eps_lin_gelu_kernel(tc, xT, w_words, w_scales, b, offs, out):
 
         out_rows = out.rearrange("(h p) c -> p h c", h=2)
         results = {}
-        for rank, e0, count in ((0, 0, 4), (0, 4, 4), (1, 0, 2), (1, 2, 3), (1, 5, 3)):
+        for rank, e0, count in ((0, 0, 4), (0, 4, 4), (1, 0, 2), (1, 2, 3), (1, 5, 1), (1, 6, 2)):
             result = keep.tile([P, 2, count * U], F32, name="result%d_%d" % (rank, e0), align_bytes=1024)
             for k in range(count):
                 results[(rank, e0 + k)] = (result, k)
 
-        def activate(blocks):
+        def activate(blocks, halves=(0, 1)):
             for k0 in range(0, len(blocks), 2):
-                for h in range(2):
+                for h in halves:
                     for rank, e in blocks[k0 : k0 + 2]:
                         result, k = results[(rank, e)]
                         nc.scalar.activation(
@@ -189,37 +189,38 @@ def tile_moe_eps_lin_gelu_kernel(tc, xT, w_words, w_scales, b, offs, out):
         woven = raw_late[-1][0][:].bitcast(BF16)
         later = keep.tile([P, 3 * block], BF16, name="later", align_bytes=256)
         gather(small, 0)
-        weave(small, 0, woven[:, : 2 * block], "gpsimd")
+        weave(small, 0, 0, 2, woven[:, : 2 * block], "gpsimd")
         gather(mid, 0)
-        weave(mid, 0, woven[:, 2 * block : 5 * block], "gpsimd")
+        weave(mid, 0, 0, 3, woven[:, 2 * block : 5 * block], "gpsimd")
         gather(last, 0)
         for room, rows, t0, n in raw_late:
             cast(seconds[:, HALF + t0 : HALF + t0 + n, :], rows, 0)
-        weave(last, 0, woven[:, 5 * block : 8 * block], "scalar")
+        weave(last, 0, 0, 3, woven[:, 5 * block : 8 * block], "scalar")
+        both = slice(0, 2)
         multiply(woven[:, : 4 * block], [(0, 0), (0, 1), (0, 2), (0, 3)])
         gather(mid, 2)
-        weave(mid, 1, later[:], "gpsimd")
+        weave(mid, 1, 0, 3, later[:], "gpsimd")
         multiply(woven[:, 4 * block : 8 * block], [(0, 4), (0, 5), (0, 6), (0, 7)])
         gather(last, 2)
         activate([(0, 0), (0, 1), (0, 2), (0, 3)])
-        store(0, 0, slice(0, 2))
+        store(0, 0, both)
         activate([(0, 4), (0, 5), (0, 6), (0, 7)])
-        store(0, 4, slice(0, 2))
+        store(0, 4, both)
         multiply(later[:, : 2 * block], [(1, 2), (1, 3)])
         multiply(later[:, 2 * block :], [(1, 4)])
-        weave(last, 1, later[:], "gpsimd")
+        weave(last, 1, 0, 3, later[:], "gpsimd")
         gather(small, 2)
         activate([(1, 2), (1, 3)])
         activate([(1, 4)])
-        store(1, 2, slice(0, 2))
-        multiply(later[:, : 2 * block], [(1, 5), (1, 6)])
+        store(1, 2, both)
         final = held_b[:, 0, : 2 * C].bitcast(BF16)
-        weave(small, 1, final, "vector")
-        multiply(later[:, 2 * block :], [(1, 7)])
+        multiply(later[:, :block], [(1, 5)])
+        weave(small, 1, 0, 2, final, "vector")
+        multiply(later[:, block:], [(1, 6), (1, 7)])
         multiply(final, [(1, 0), (1, 1)])
-        activate([(1, 5), (1, 6)])
-        activate([(1, 7)])
-        store(1, 5, slice(0, 2))
-        activate([(1, 0), (1, 1)])
-        store(1, 0, slice(0, 1))
-        store(1, 0, slice(1, 2))
+        activate([(1, 5)])
+        store(1, 5, both)
+        for e0 in (6, 0):
+            for h in range(2):
+                activate([(1, e0), (1, e0 + 1)], (h,))
+                store(1, e0, slice(h, h + 1))

@@ -26,6 +26,7 @@ FIRST_CUTS = ((1664, 1112), (1152, 768), (768, 512), (512, 344))
 LATE_CUTS = (768, 768, 512)
 GROUP = 16
 ROW = 3 * C
+SET = 4
 
 
 def tile_moe_eps_lin_gelu_kernel(tc, xT, w_words, w_scales, b, offs, out):
@@ -35,8 +36,8 @@ def tile_moe_eps_lin_gelu_kernel(tc, xT, w_words, w_scales, b, offs, out):
         psum = ctx.enter_context(tc.psum_pool(name="psum", bufs=1))
 
         offsets = keep.tile([P, S // GROUP], U16, name="offsets")
-        w_sb = keep.tile([P, E, 2 * N], U8, name="w_sb", align_bytes=512)
-        ws_sb = keep.tile([P, E * N], U8, name="ws_sb", align_bytes=256)
+        w_sb = [keep.tile([P, SET, 2 * N], U8, name="w_sb%d" % i, align_bytes=512) for i in range(E // SET)]
+        ws_sb = [keep.tile([P, SET * N], U8, name="ws_sb%d" % i, align_bytes=256) for i in range(E // SET)]
         bias = keep.tile([P, 2, E], F32, name="bias")
         warm = keep.tile([P, 1], F32, name="warm")
 
@@ -66,16 +67,19 @@ def tile_moe_eps_lin_gelu_kernel(tc, xT, w_words, w_scales, b, offs, out):
 
         nc.vector.memset(warm[:], 0.0)
         nc.scalar.activation(warm[:], warm[:], ACT.Gelu_apprx_tanh)
-        nc.vector.memset(ws_sb[:].bitcast(I32), 0)
-        for q in range(4):
+        for i in range(E // SET):
+            experts = slice(SET * i, SET * (i + 1))
+            nc.vector.memset(ws_sb[i][:].bitcast(I32), 0)
+            for q in range(4):
+                nc.sync.dma_start(
+                    out=ws_sb[i][32 * q : 32 * q + 4, :].rearrange("q (e n) -> q e n", e=SET).bitcast(I32),
+                    in_=w_scales[experts, 0, 4 * q : 4 * q + 4, :].rearrange("e q n -> q e n").bitcast(I32),
+                )
             nc.sync.dma_start(
-                out=ws_sb[32 * q : 32 * q + 4, :].rearrange("q (e n) -> q e n", e=E).bitcast(I32),
-                in_=w_scales[:, 0, 4 * q : 4 * q + 4, :].rearrange("e q n -> q e n").bitcast(I32),
+                out=w_sb[i][:].bitcast(I32), in_=w_words[experts].rearrange("e a p c -> p (e a) c").bitcast(I32)
             )
-        nc.sync.dma_start(
-            out=w_sb[:].bitcast(I32), in_=w_words.rearrange("e a p c -> p (e a) c").bitcast(I32)
-        )
-        nc.sync.dma_start(out=bias[:], in_=b.rearrange("(h p) e -> p h e", h=2))
+            if i == 0:
+                nc.sync.dma_start(out=bias[:], in_=b.rearrange("(h p) e -> p h e", h=2))
 
         seconds = keep.tile([P, 3 * HALF, 2], BF16, name="seconds", align_bytes=256)
         firsts = keep.tile([P, T, 2], BF16, name="firsts", align_bytes=256)
@@ -128,9 +132,8 @@ def tile_moe_eps_lin_gelu_kernel(tc, xT, w_words, w_scales, b, offs, out):
                 )
 
         sums = {}
-        turn = [0]
 
-        def multiply(values, blocks):
+        def multiply(values, blocks, first_bank):
             n = U * len(blocks)
             name = "%d_%d" % blocks[0]
             codes = keep.tile([P, n], U32, name="codes" + name, align_bytes=256)
@@ -138,15 +141,14 @@ def tile_moe_eps_lin_gelu_kernel(tc, xT, w_words, w_scales, b, offs, out):
             nc.vector.quantize_mx(out=codes[:].bitcast(FP8X4), scales=scales[:], in_=values)
             for k0 in range(0, len(blocks), 2):
                 for h in range(2):
-                    bank = psum.tile([P, 2, U], F32, name="bank%d" % (turn[0] % 8))
-                    turn[0] = turn[0] + 1
+                    bank = psum.tile([P, 2, U], F32, name="bank%d" % (first_bank + k0 + h))
                     for k in range(k0, min(k0 + 2, len(blocks))):
                         rank, e = blocks[k]
                         sums[(rank, e, h)] = bank[:, k - k0, :]
                         nc.tensor.matmul_mx(
                             out=bank[:, k - k0, :],
-                            lhsT=w_sb[:, e, 256 * h : 256 * h + 256].bitcast(FP4X4),
-                            lhsT_scale=ws_sb[:, e * N + 128 * h : e * N + 128 * h + 128],
+                            lhsT=w_sb[e // SET][:, e % SET, 256 * h : 256 * h + 256].bitcast(FP4X4),
+                            lhsT_scale=ws_sb[e // SET][:, e % SET * N + 128 * h : e % SET * N + 128 * h + 128],
                             rhs=codes[:, k * U : (k + 1) * U].bitcast(FP8X4),
                             rhs_scale=scales[:, k * U : (k + 1) * U],
                             start=True,
@@ -195,29 +197,29 @@ def tile_moe_eps_lin_gelu_kernel(tc, xT, w_words, w_scales, b, offs, out):
         gather(last, 0)
         for room, rows, t0, n in raw_late:
             cast(seconds[:, HALF + t0 : HALF + t0 + n, :], rows, 0)
-        weave(last, 0, 0, 3, woven[:, 5 * block : 8 * block], "scalar")
+        weave(last, 0, 0, 3, woven[:, 5 * block : 8 * block], "gpsimd")
         both = slice(0, 2)
-        multiply(woven[:, : 4 * block], [(0, 0), (0, 1), (0, 2), (0, 3)])
+        multiply(woven[:, : 4 * block], [(0, 0), (0, 1), (0, 2), (0, 3)], 0)
         gather(mid, 2)
         weave(mid, 1, 0, 3, later[:], "gpsimd")
-        multiply(woven[:, 4 * block : 8 * block], [(0, 4), (0, 5), (0, 6), (0, 7)])
+        multiply(woven[:, 4 * block : 8 * block], [(0, 4), (0, 5), (0, 6), (0, 7)], 4)
         gather(last, 2)
         activate([(0, 0), (0, 1), (0, 2), (0, 3)])
         store(0, 0, both)
         activate([(0, 4), (0, 5), (0, 6), (0, 7)])
         store(0, 4, both)
-        multiply(later[:, : 2 * block], [(1, 2), (1, 3)])
-        multiply(later[:, 2 * block :], [(1, 4)])
+        multiply(later[:, : 2 * block], [(1, 2), (1, 3)], 4)
+        multiply(later[:, 2 * block :], [(1, 4)], 6)
         weave(last, 1, 0, 3, later[:], "gpsimd")
         gather(small, 2)
         activate([(1, 2), (1, 3)])
         activate([(1, 4)])
         store(1, 2, both)
         final = held_b[:, 0, : 2 * C].bitcast(BF16)
-        multiply(later[:, :block], [(1, 5)])
+        multiply(later[:, :block], [(1, 5)], 4)
         weave(small, 1, 0, 2, final, "vector")
-        multiply(later[:, block:], [(1, 6), (1, 7)])
-        multiply(final, [(1, 0), (1, 1)])
+        multiply(later[:, block:], [(1, 6), (1, 7)], 6)
+        multiply(final, [(1, 0), (1, 1)], 4)
         activate([(1, 5)])
         store(1, 5, both)
         for e0 in (6, 0):

@@ -23,7 +23,8 @@ ACT = mybir.ActivationFunctionType
 
 EARLY_VECTOR = 1360
 FIRST_CUTS = ((1664, 1112), (1152, 768), (768, 512), (512, 344))
-LATE_CUTS = (768, 768, 512)
+LATE_CUTS = (1280, 768)
+LATE_GPSIMD = (384, 256)
 GROUP = 16
 ROW = 3 * C
 SET = 4
@@ -36,7 +37,7 @@ def tile_moe_eps_lin_gelu_kernel(tc, xT, w_words, w_scales, b, offs, out):
         psum = ctx.enter_context(tc.psum_pool(name="psum", bufs=1))
 
         offsets = keep.tile([P, S // GROUP], U16, name="offsets")
-        w_sb = [keep.tile([P, SET, 2 * N], U8, name="w_sb%d" % i, align_bytes=512) for i in range(E // SET)]
+        w_sb = [keep.tile([P, 2, 2 * N], U8, name="w_sb%d" % i, align_bytes=512) for i in range(E // 2)]
         ws_sb = [keep.tile([P, SET * N], U8, name="ws_sb%d" % i, align_bytes=256) for i in range(E // SET)]
         bias = keep.tile([P, 2, E], F32, name="bias")
         warm = keep.tile([P, 1], F32, name="warm")
@@ -58,7 +59,7 @@ def tile_moe_eps_lin_gelu_kernel(tc, xT, w_words, w_scales, b, offs, out):
         raw_late = []
         t0 = HALF
         for i, n in enumerate(LATE_CUTS):
-            skip = 5 * C if i == len(LATE_CUTS) - 1 else 0
+            skip = 4 * C - LATE_GPSIMD[0] if i == 0 else 0
             room = keep.tile([P, skip + 2 * n], F32, name="raw_late%d" % i, align_bytes=1024)
             rows = room[:, skip:].rearrange("p (j t) -> p j t", j=2)
             nc.sync.dma_start(out=rows, in_=x_rows[:, 2:4, t0 : t0 + n])
@@ -75,11 +76,13 @@ def tile_moe_eps_lin_gelu_kernel(tc, xT, w_words, w_scales, b, offs, out):
                     out=ws_sb[i][32 * q : 32 * q + 4, :].rearrange("q (e n) -> q e n", e=SET).bitcast(I32),
                     in_=w_scales[experts, 0, 4 * q : 4 * q + 4, :].rearrange("e q n -> q e n").bitcast(I32),
                 )
-            nc.sync.dma_start(
-                out=w_sb[i][:].bitcast(I32), in_=w_words[experts].rearrange("e a p c -> p (e a) c").bitcast(I32)
-            )
-            if i == 0:
-                nc.sync.dma_start(out=bias[:], in_=b.rearrange("(h p) e -> p h e", h=2))
+            for j in (2 * i, 2 * i + 1):
+                nc.sync.dma_start(
+                    out=w_sb[j][:].bitcast(I32),
+                    in_=w_words[2 * j : 2 * j + 2].rearrange("e a p c -> p (e a) c").bitcast(I32),
+                )
+                if j == 0:
+                    nc.sync.dma_start(out=bias[:], in_=b.rearrange("(h p) e -> p h e", h=2))
 
         seconds = keep.tile([P, 3 * HALF, 2], BF16, name="seconds", align_bytes=256)
         firsts = keep.tile([P, T, 2], BF16, name="firsts", align_bytes=256)
@@ -147,7 +150,7 @@ def tile_moe_eps_lin_gelu_kernel(tc, xT, w_words, w_scales, b, offs, out):
                         sums[(rank, e, h)] = bank[:, k - k0, :]
                         nc.tensor.matmul_mx(
                             out=bank[:, k - k0, :],
-                            lhsT=w_sb[e // SET][:, e % SET, 256 * h : 256 * h + 256].bitcast(FP4X4),
+                            lhsT=w_sb[e // 2][:, e % 2, 256 * h : 256 * h + 256].bitcast(FP4X4),
                             lhsT_scale=ws_sb[e // SET][:, e % SET * N + 128 * h : e % SET * N + 128 * h + 128],
                             rhs=codes[:, k * U : (k + 1) * U].bitcast(FP8X4),
                             rhs_scale=scales[:, k * U : (k + 1) * U],
@@ -188,21 +191,35 @@ def tile_moe_eps_lin_gelu_kernel(tc, xT, w_words, w_scales, b, offs, out):
         for n, v in FIRST_CUTS:
             cast(firsts[:, t0 : t0 + n, :], first_rows[:, :, t0 : t0 + n], v)
             t0 = t0 + n
-        woven = raw_late[-1][0][:].bitcast(BF16)
+        woven = raw_late[0][0][:].bitcast(BF16)[:, : 4 * block]
         later = keep.tile([P, 3 * block], BF16, name="later", align_bytes=256)
+        def cast_late(i, engine):
+            room, rows, t0, n = raw_late[i]
+            g = LATE_GPSIMD[i]
+            if engine == "gpsimd":
+                nc.gpsimd.tensor_copy(
+                    seconds[:, HALF + t0 : HALF + t0 + g, :], rows[:, :, :g].rearrange("p j t -> p t j")
+                )
+            else:
+                cast(seconds[:, HALF + t0 + g : HALF + t0 + n, :], rows[:, :, g:], 0)
+
+        late_room = raw_late[1][0][:].bitcast(BF16)
         gather(small, 0)
         weave(small, 0, 0, 2, woven[:, : 2 * block], "gpsimd")
         gather(mid, 0)
-        weave(mid, 0, 0, 3, woven[:, 2 * block : 5 * block], "gpsimd")
+        cast_late(0, "gpsimd")
+        cast_late(0, "scalar")
+        weave(mid, 0, 0, 2, woven[:, 2 * block :], "gpsimd")
         gather(last, 0)
-        for room, rows, t0, n in raw_late:
-            cast(seconds[:, HALF + t0 : HALF + t0 + n, :], rows, 0)
-        weave(last, 0, 0, 3, woven[:, 5 * block : 8 * block], "gpsimd")
+        cast_late(1, "gpsimd")
+        cast_late(1, "scalar")
+        weave(mid, 0, 2, 3, late_room[:, :block], "scalar")
+        weave(last, 0, 0, 3, late_room[:, block : 4 * block], "gpsimd")
         both = slice(0, 2)
-        multiply(woven[:, : 4 * block], [(0, 0), (0, 1), (0, 2), (0, 3)], 0)
+        multiply(woven, [(0, 0), (0, 1), (0, 2), (0, 3)], 0)
         gather(mid, 2)
         weave(mid, 1, 0, 3, later[:], "gpsimd")
-        multiply(woven[:, 4 * block : 8 * block], [(0, 4), (0, 5), (0, 6), (0, 7)], 4)
+        multiply(late_room[:, : 4 * block], [(0, 4), (0, 5), (0, 6), (0, 7)], 4)
         gather(last, 2)
         activate([(0, 0), (0, 1), (0, 2), (0, 3)])
         store(0, 0, both)
@@ -217,8 +234,8 @@ def tile_moe_eps_lin_gelu_kernel(tc, xT, w_words, w_scales, b, offs, out):
         store(1, 2, both)
         final = held_b[:, 0, : 2 * C].bitcast(BF16)
         multiply(later[:, :block], [(1, 5)], 4)
-        weave(small, 1, 0, 2, final, "vector")
         multiply(later[:, block:], [(1, 6), (1, 7)], 6)
+        weave(small, 1, 0, 2, final, "vector")
         multiply(final, [(1, 0), (1, 1)], 4)
         activate([(1, 5)])
         store(1, 5, both)

@@ -40,7 +40,6 @@ def tile_moe_eps_lin_gelu_kernel(tc, xT, w_words, w_scales, b, offs, out):
         w_sb = [keep.tile([P, 2, 2 * N], U8, name="w_sb%d" % i, align_bytes=512) for i in range(E // 2)]
         ws_sb = [keep.tile([P, SET * N], U8, name="ws_sb%d" % i, align_bytes=256) for i in range(E // SET)]
         bias = keep.tile([P, 2, E], F32, name="bias")
-        warm = keep.tile([P, 1], F32, name="warm")
 
         x_rows = xT.rearrange("(p j) t -> p j t", j=PACK)
         x_flat = xT.rearrange("(p j) t -> p (j t)", j=PACK)
@@ -66,15 +65,13 @@ def tile_moe_eps_lin_gelu_kernel(tc, xT, w_words, w_scales, b, offs, out):
             raw_late.append((room, rows, t0, n))
             t0 = t0 + n
 
-        nc.vector.memset(warm[:], 0.0)
-        nc.scalar.activation(warm[:], warm[:], ACT.Gelu_apprx_tanh)
         for i in range(E // SET):
             experts = slice(SET * i, SET * (i + 1))
             nc.vector.memset(ws_sb[i][:].bitcast(I32), 0)
             for q in range(4):
                 nc.sync.dma_start(
-                    out=ws_sb[i][32 * q : 32 * q + 4, :].rearrange("q (e n) -> q e n", e=SET).bitcast(I32),
-                    in_=w_scales[experts, 0, 4 * q : 4 * q + 4, :].rearrange("e q n -> q e n").bitcast(I32),
+                    out=ws_sb[i][q:P:32, :].rearrange("q (e n) -> q e n", e=SET).bitcast(I32),
+                    in_=w_scales[experts, 0, q:16:4, :].rearrange("e q n -> q e n").bitcast(I32),
                 )
             for j in (2 * i, 2 * i + 1):
                 nc.sync.dma_start(
@@ -160,7 +157,7 @@ def tile_moe_eps_lin_gelu_kernel(tc, xT, w_words, w_scales, b, offs, out):
 
         out_rows = out.rearrange("(h p) c -> p h c", h=2)
         results = {}
-        for rank, e0, count in ((0, 0, 4), (0, 4, 4), (1, 0, 2), (1, 2, 3), (1, 5, 1), (1, 6, 2)):
+        for rank, e0, count in ((0, 0, 4), (0, 4, 4), (1, 0, 1), (1, 1, 1), (1, 2, 3), (1, 5, 1), (1, 6, 2)):
             result = keep.tile([P, 2, count * U], F32, name="result%d_%d" % (rank, e0), align_bytes=1024)
             for k in range(count):
                 results[(rank, e0 + k)] = (result, k)
@@ -236,10 +233,13 @@ def tile_moe_eps_lin_gelu_kernel(tc, xT, w_words, w_scales, b, offs, out):
         multiply(later[:, :block], [(1, 5)], 4)
         multiply(later[:, block:], [(1, 6), (1, 7)], 6)
         weave(small, 1, 0, 2, final, "vector")
-        multiply(final, [(1, 0), (1, 1)], 4)
+        multiply(final[:, :block], [(1, 0)], 4)
         activate([(1, 5)])
         store(1, 5, both)
-        for e0 in (6, 0):
-            for h in range(2):
-                activate([(1, e0), (1, e0 + 1)], (h,))
-                store(1, e0, slice(h, h + 1))
+        for h in range(2):
+            activate([(1, 6), (1, 7)], (h,))
+            store(1, 6, slice(h, h + 1))
+        multiply(final[:, block:], [(1, 1)], 6)
+        for e in range(2):
+            activate([(1, e)])
+            store(1, e, both)

@@ -21,13 +21,14 @@ FP8X4 = mybir.dt.float8_e4m3fn_x4
 FP4X4 = mybir.dt.float4_e2m1fn_x4
 ACT = mybir.ActivationFunctionType
 
-EARLY_VECTOR = 1360
-FIRST_CUTS = ((1664, 1112), (1152, 768), (768, 512), (512, 344))
-LATE_CUTS = (1280, 768)
-LATE_GPSIMD = (384, 256)
 GROUP = 16
-ROW = 3 * C
-SET = 4
+EARLY = 2
+TABLES = (
+    (1, 0, True, ((1280, 856, 0), (768, 512, 0))),
+    (1, 1, False, ((1024, 0, 0), (1024, 680, 0))),
+    (0, 0, False, ((1024, 0, 0), (1024, 0, 0))),
+    (0, 1, False, ((960, 0, 400), (704, 0, 288), (384, 0, 160))),
+)
 
 
 def tile_moe_eps_lin_gelu_kernel(tc, xT, w_words, w_scales, b, offs, out):
@@ -37,209 +38,207 @@ def tile_moe_eps_lin_gelu_kernel(tc, xT, w_words, w_scales, b, offs, out):
         psum = ctx.enter_context(tc.psum_pool(name="psum", bufs=1))
 
         offsets = keep.tile([P, S // GROUP], U16, name="offsets")
-        w_sb = [keep.tile([P, 2, 2 * N], U8, name="w_sb%d" % i, align_bytes=512) for i in range(E // 2)]
-        ws_sb = [keep.tile([P, SET * N], U8, name="ws_sb%d" % i, align_bytes=256) for i in range(E // SET)]
-        bias = keep.tile([P, 2, E], F32, name="bias")
-
         x_rows = xT.rearrange("(p j) t -> p j t", j=PACK)
-        x_flat = xT.rearrange("(p j) t -> p (j t)", j=PACK)
 
-        raw_early = keep.tile([P, 2, HALF], F32, name="raw_early", align_bytes=1024)
-        nc.sync.dma_start(out=raw_early[:], in_=x_rows[:, 2:4, 0:HALF])
-        nc.sync.dma_start(offsets[:], offs)
-        raw_first = keep.tile([P, 2 * T], F32, name="raw_first", align_bytes=1024)
-        begin = 0
-        t0 = 0
-        for n, v in FIRST_CUTS:
-            end = T + t0 + n
-            nc.sync.dma_start(out=raw_first[:, begin:end], in_=x_flat[:, begin:end])
-            begin = end
-            t0 = t0 + n
-        raw_late = []
-        t0 = HALF
-        for i, n in enumerate(LATE_CUTS):
-            skip = 4 * C - LATE_GPSIMD[0] if i == 0 else 0
-            room = keep.tile([P, skip + 2 * n], F32, name="raw_late%d" % i, align_bytes=1024)
-            rows = room[:, skip:].rearrange("p (j t) -> p j t", j=2)
-            nc.sync.dma_start(out=rows, in_=x_rows[:, 2:4, t0 : t0 + n])
-            raw_late.append((room, rows, t0, n))
-            t0 = t0 + n
+        warm_in = keep.tile([P, 1], F32, name="warm_in")
+        warm_out = keep.tile([P, 1], F32, name="warm_out")
+        nc.gpsimd.memset(warm_in[:], 0.0)
+        nc.scalar.activation(warm_out[:], warm_in[:], ACT.Gelu_apprx_tanh)
 
-        for i in range(E // SET):
-            experts = slice(SET * i, SET * (i + 1))
-            nc.vector.memset(ws_sb[i][:].bitcast(I32), 0)
+        w_codes = {}
+        w_planes = {}
+
+        def load_scales(e0, count):
+            plane = keep.tile([P, count * N], U8, name="plane%d" % e0, align_bytes=256)
+            nc.gpsimd.memset(plane[:].bitcast(I32), 0)
             for q in range(4):
                 nc.sync.dma_start(
-                    out=ws_sb[i][q:P:32, :].rearrange("q (e n) -> q e n", e=SET).bitcast(I32),
-                    in_=w_scales[experts, 0, q:16:4, :].rearrange("e q n -> q e n").bitcast(I32),
+                    out=plane[q:P:32, :].rearrange("q (e n) -> q e n", e=count).bitcast(I32),
+                    in_=w_scales[e0 : e0 + count, 0, q:16:4, :].rearrange("e q n -> q e n").bitcast(I32),
                 )
-            for j in (2 * i, 2 * i + 1):
-                nc.sync.dma_start(
-                    out=w_sb[j][:].bitcast(I32),
-                    in_=w_words[2 * j : 2 * j + 2].rearrange("e a p c -> p (e a) c").bitcast(I32),
-                )
-                if j == 0:
-                    nc.sync.dma_start(out=bias[:], in_=b.rearrange("(h p) e -> p h e", h=2))
+            for k in range(count):
+                w_planes[e0 + k] = plane[:, k * N : (k + 1) * N]
 
-        seconds = keep.tile([P, 3 * HALF, 2], BF16, name="seconds", align_bytes=256)
-        firsts = keep.tile([P, T, 2], BF16, name="firsts", align_bytes=256)
-        second_words = seconds[:].rearrange("p t j -> p (t j)").bitcast(U32)
-        first_words = firsts[:].rearrange("p t j -> p (t j)").bitcast(U32)
-        nc.vector.memset(seconds[:, HALF:T, :].rearrange("p t j -> p (t j)").bitcast(I32), 0)
+        def load_words(e0):
+            words = keep.tile([P, 2, 2 * N], U8, name="words%d" % e0, align_bytes=512)
+            nc.sync.dma_start(
+                out=words[:].bitcast(I32),
+                in_=w_words[e0 : e0 + 2].rearrange("e a p c -> p (e a) c").bitcast(I32),
+            )
+            for k in range(2):
+                w_codes[e0 + k] = words[:, k, :]
 
-        def cast(table, rows, v):
-            n = rows.shape[2]
-            dst = table.rearrange("p (c i) j -> p c j i", i=4)
-            src = rows.rearrange("p j (c i) -> p c j i", i=4)
-            if v > 0:
-                nc.vector.tensor_copy(out=dst[:, : v // 4], in_=src[:, : v // 4])
-            if v < n:
-                nc.scalar.activation(dst[:, v // 4 :], src[:, v // 4 :], ACT.Copy)
+        raws = []
 
-        held_a = keep.tile([P, 5, ROW], U32, name="held_a", align_bytes=256)
-        held_b = keep.tile([P, 2, ROW], U32, name="held_b", align_bytes=256)
-        small = (0, 2, held_a, 2, 3, 4)
-        mid = (2, 3, held_a, 0, 1, 4)
-        last = (5, 3, held_b, 0, 1, 1)
+        def load_rows(i):
+            rank, pair, whole, cuts = TABLES[i]
+            source = x_rows[:, 2 * pair : 2 * pair + 2, rank * HALF : (rank + 1) * HALF]
+            pieces = []
+            if whole:
+                raw = keep.tile([P, 2 * HALF], F32, name="raw%d" % i, align_bytes=1024)
+                nc.sync.dma_start(out=raw[:, :HALF], in_=source[:, 0, :])
+            if i == 0:
+                nc.sync.dma_start(offsets[:], offs)
+            t0 = 0
+            for n, v, g in cuts:
+                if whole:
+                    nc.sync.dma_start(out=raw[:, HALF + t0 : HALF + t0 + n], in_=source[:, 1, t0 : t0 + n])
+                    pieces.append(raw[:].rearrange("p (j t) -> p j t", j=2)[:, :, t0 : t0 + n])
+                else:
+                    piece = keep.tile([P, 2, n], F32, name="raw%d_%d" % (i, t0), align_bytes=1024)
+                    nc.sync.dma_start(out=piece[:], in_=source[:, :, t0 : t0 + n])
+                    pieces.append(piece[:])
+                t0 = t0 + n
+            raws.append(pieces)
 
-        def gather(group, which):
-            e0, count, held = group[:3]
-            lo, hi = 0, count * C
-            if count == 3 and which == 1:
-                hi = hi - U
-            if count == 3 and which == 2:
-                lo = U
-            window = (first_words, second_words[:, :T], second_words[:, HALF:])[which]
-            entries = offsets[:, (e0 * C + lo) // GROUP : (e0 * C + hi) // GROUP]
-            nc.vector.tensor_copy(held[:, group[3 + which], lo:hi], window.indirect(entries))
+        bias = keep.tile([P, 2, E], F32, name="bias")
+        for i in range(3):
+            load_rows(i)
+        load_scales(0, EARLY)
+        nc.sync.dma_start(out=bias[:], in_=b.rearrange("(h p) e -> p h e", h=2))
+        for e0 in range(0, EARLY, 2):
+            load_words(e0)
+        load_rows(3)
+        load_scales(EARLY, E - EARLY)
+        for e0 in range(EARLY, E, 2):
+            load_words(e0)
 
-        def weave(group, rank, lo, hi, dst, engine):
-            held, first = group[2:4]
-            second = group[4 + rank]
-            src = held[:, first : second + 1 : second - first, lo * C : hi * C]
-            src = src.rearrange("p u (e r n) -> p r e n u", r=R, n=U)[:, rank]
-            words = dst.bitcast(U32).rearrange("p (e n u) -> p e n u", n=U, u=2)
-            if engine == "gpsimd":
-                nc.gpsimd.tensor_copy(words, src)
-            elif engine == "scalar":
-                nc.scalar.copy(words, src)
-            else:
-                nc.vector.tensor_copy(
-                    dst.bitcast(I32).rearrange("p (e n u) -> p e n u", n=U, u=2),
-                    held[:].bitcast(I32)[:, first : second + 1 : second - first, lo * C : hi * C].rearrange(
-                        "p u (e r n) -> p r e n u", r=R, n=U
-                    )[:, rank],
-                )
+        tables = []
+        for i in range(4):
+            rank = TABLES[i][0]
+            table = keep.tile([P, (rank + 1) * HALF], U32, name="table%d" % i, align_bytes=256)
+            if rank == 1:
+                nc.vector.memset(table[:, :HALF].bitcast(I32), 0)
+            tables.append(table)
 
-        sums = {}
+        def round_rows(i):
+            rank, pair, whole, cuts = TABLES[i]
+            pairs = tables[i][:, rank * HALF :].bitcast(BF16).rearrange("p (c i j) -> p c j i", i=4, j=2)
+            t0 = 0
+            for (n, v, g), piece in zip(cuts, raws[i]):
+                rows = piece.rearrange("p j (c i) -> p c j i", i=4)
+                part = pairs[:, t0 // 4 : (t0 + n) // 4]
+                mid, late = v // 4, (n - g) // 4
+                if v > 0:
+                    nc.vector.tensor_copy(out=part[:, :mid], in_=rows[:, :mid])
+                nc.scalar.activation(part[:, mid:late], rows[:, mid:late], ACT.Copy)
+                if g > 0:
+                    nc.gpsimd.tensor_copy(
+                        part[:, late:].rearrange("p c j i -> p c i j"), rows[:, late:].rearrange("p c j i -> p c i j")
+                    )
+                t0 = t0 + n
 
-        def multiply(values, blocks, first_bank):
-            n = U * len(blocks)
-            name = "%d_%d" % blocks[0]
-            codes = keep.tile([P, n], U32, name="codes" + name, align_bytes=256)
-            scales = keep.tile([P, n], U8, name="scales" + name, align_bytes=256)
+        held1 = [keep.tile([P, 2, 3 * U], U32, name="held1_%d" % g, align_bytes=256) for g in range(E // 2)]
+        both0 = [keep.tile([P, 2, 2, U], U32, name="held0_%d" % g, align_bytes=256) for g in range(E // 2)]
+        held0 = [both0[e // 2][:, e % 2] for e in range(E)]
+
+        def gather(i, held, first, count):
+            entries = offsets[:, first // GROUP : (first + count) // GROUP]
+            nc.vector.tensor_copy(held[:, TABLES[i][1], :], tables[i][:].indirect(entries))
+
+        tokens = {}
+
+        def quantise(values, rank, e0):
+            n = values.shape[1] // PACK
+            codes = keep.tile([P, n], U32, name="codes%d_%d" % (rank, e0), align_bytes=256)
+            scales = keep.tile([P, n], U8, name="scales%d_%d" % (rank, e0), align_bytes=256)
             nc.vector.quantize_mx(out=codes[:].bitcast(FP8X4), scales=scales[:], in_=values)
-            for k0 in range(0, len(blocks), 2):
-                for h in range(2):
-                    bank = psum.tile([P, 2, U], F32, name="bank%d" % (first_bank + k0 + h))
-                    for k in range(k0, min(k0 + 2, len(blocks))):
-                        rank, e = blocks[k]
-                        sums[(rank, e, h)] = bank[:, k - k0, :]
-                        nc.tensor.matmul_mx(
-                            out=bank[:, k - k0, :],
-                            lhsT=w_sb[e // 2][:, e % 2, 256 * h : 256 * h + 256].bitcast(FP4X4),
-                            lhsT_scale=ws_sb[e // SET][:, e % SET * N + 128 * h : e % SET * N + 128 * h + 128],
-                            rhs=codes[:, k * U : (k + 1) * U].bitcast(FP8X4),
-                            rhs_scale=scales[:, k * U : (k + 1) * U],
-                            start=True,
-                            stop=True,
-                        )
+            for k in range(n // U):
+                tokens[(rank, e0 + k)] = (codes[:, k * U : (k + 1) * U], scales[:, k * U : (k + 1) * U])
 
         out_rows = out.rearrange("(h p) c -> p h c", h=2)
         results = {}
-        for rank, e0, count in ((0, 0, 4), (0, 4, 4), (1, 0, 1), (1, 1, 1), (1, 2, 3), (1, 5, 1), (1, 6, 2)):
-            result = keep.tile([P, 2, count * U], F32, name="result%d_%d" % (rank, e0), align_bytes=1024)
-            for k in range(count):
-                results[(rank, e0 + k)] = (result, k)
+        for rank in range(R):
+            for e0, count in ((0, 2), (2, 2), (4, 2), (6, 2)) if rank == 1 else ((0, 2), (2, 2), (4, 2), (6, 1), (7, 1)):
+                result = keep.tile([P, 2, count * U], F32, name="result%d_%d" % (rank, e0), align_bytes=1024)
+                for k in range(count):
+                    results[(rank, e0 + k)] = (result, k, e0)
 
-        def activate(blocks, halves=(0, 1)):
-            for k0 in range(0, len(blocks), 2):
-                for h in halves:
-                    for rank, e in blocks[k0 : k0 + 2]:
-                        result, k = results[(rank, e)]
-                        nc.scalar.activation(
-                            result[:, h, k * U : (k + 1) * U],
-                            sums[(rank, e, h)],
-                            ACT.Gelu_apprx_tanh,
-                            bias=bias[:, h, e : e + 1],
-                        )
+        def finish(rank, experts, bank_number):
+            bank = psum.tile([P, len(experts), 2, U], F32, name="bank%d" % bank_number)
+            for i, e in enumerate(experts):
+                codes, scales = tokens[(rank, e)]
+                for h in range(2):
+                    nc.tensor.matmul_mx(
+                        out=bank[:, i, h, :],
+                        lhsT=w_codes[e][:, 256 * h : 256 * h + 256].bitcast(FP4X4),
+                        lhsT_scale=w_planes[e][:, 128 * h : 128 * h + 128],
+                        rhs=codes.bitcast(FP8X4),
+                        rhs_scale=scales,
+                        start=True,
+                        stop=True,
+                    )
+            for i, e in enumerate(experts):
+                result, k, e0 = results[(rank, e)]
+                for h in range(2):
+                    nc.scalar.activation(
+                        result[:, h, k * U : (k + 1) * U],
+                        bank[:, i, h, :],
+                        ACT.Gelu_apprx_tanh,
+                        bias=bias[:, h, e : e + 1],
+                    )
+                if (k + 1) * U == result.shape[2]:
+                    c0 = rank * (S // R) + e0 * U
+                    nc.sync.dma_start(out=out_rows[:, :, c0 : c0 + result.shape[2]], in_=result[:])
 
-        def store(rank, e0, halves):
-            result = results[(rank, e0)][0]
-            c0 = rank * (S // R) + e0 * U
-            nc.sync.dma_start(out=out_rows[:, halves, c0 : c0 + result.shape[2]], in_=result[:, halves, :])
+        round_rows(0)
+        for g in range(E // 2):
+            gather(0, held1[g], 2 * g * C + U, 3 * U)
+        round_rows(1)
+        woven1 = [keep.tile([P, 4 * PACK * U], BF16, name="woven1_%d" % a, align_bytes=256) for a in range(2)]
+        for g in range(E // 2):
+            gather(1, held1[g], 2 * g * C + U, 3 * U)
+            words = woven1[g // 2][:, g % 2 * 2 * PACK * U : (g % 2 + 1) * 2 * PACK * U].bitcast(U32)
+            nc.gpsimd.tensor_copy(
+                words.rearrange("p (e n u) -> p e n u", e=2, u=2),
+                held1[g][:].rearrange("p u (b n) -> p b n u", n=U)[:, 0:3:2],
+            )
+        quantise(woven1[0][:], 1, 0)
+        round_rows(2)
+        quantise(woven1[1][:], 1, 4)
+        for e in range(E):
+            gather(2, held0[e], e * C, U)
+        finish(1, (0, 1), 0)
+        round_rows(3)
+        for g in range(1, E // 2):
+            finish(1, (2 * g, 2 * g + 1), g)
 
-        block = PACK * U
-        cast(seconds[:, :HALF, :], raw_early[:], EARLY_VECTOR)
-        for group in (small, mid, last):
-            gather(group, 1)
-        first_rows = raw_first[:].rearrange("p (j t) -> p j t", j=2)
-        t0 = 0
-        for n, v in FIRST_CUTS:
-            cast(firsts[:, t0 : t0 + n, :], first_rows[:, :, t0 : t0 + n], v)
-            t0 = t0 + n
-        woven = raw_late[0][0][:].bitcast(BF16)[:, : 4 * block]
-        later = keep.tile([P, 3 * block], BF16, name="later", align_bytes=256)
-        def cast_late(i, engine):
-            room, rows, t0, n = raw_late[i]
-            g = LATE_GPSIMD[i]
-            if engine == "gpsimd":
-                nc.gpsimd.tensor_copy(
-                    seconds[:, HALF + t0 : HALF + t0 + g, :], rows[:, :, :g].rearrange("p j t -> p t j")
-                )
-            else:
-                cast(seconds[:, HALF + t0 + g : HALF + t0 + n, :], rows[:, :, g:], 0)
+        steps = ((0, 2), (2, 2), (4, 1), (5, 1), (6, 1), (7, 1))
+        woven0 = {}
+        for e0, count in steps:
+            woven0[e0] = keep.tile([P, count * PACK * U], BF16, name="woven0_%d" % e0, align_bytes=256)
 
-        late_room = raw_late[1][0][:].bitcast(BF16)
-        gather(small, 0)
-        weave(small, 0, 0, 2, woven[:, : 2 * block], "gpsimd")
-        gather(mid, 0)
-        cast_late(0, "gpsimd")
-        cast_late(0, "scalar")
-        weave(mid, 0, 0, 2, woven[:, 2 * block :], "gpsimd")
-        gather(last, 0)
-        cast_late(1, "gpsimd")
-        cast_late(1, "scalar")
-        weave(mid, 0, 2, 3, late_room[:, :block], "scalar")
-        weave(last, 0, 0, 3, late_room[:, block : 4 * block], "gpsimd")
-        both = slice(0, 2)
-        multiply(woven, [(0, 0), (0, 1), (0, 2), (0, 3)], 0)
-        gather(mid, 2)
-        weave(mid, 1, 0, 3, later[:], "gpsimd")
-        multiply(late_room[:, : 4 * block], [(0, 4), (0, 5), (0, 6), (0, 7)], 4)
-        gather(last, 2)
-        activate([(0, 0), (0, 1), (0, 2), (0, 3)])
-        store(0, 0, both)
-        activate([(0, 4), (0, 5), (0, 6), (0, 7)])
-        store(0, 4, both)
-        multiply(later[:, : 2 * block], [(1, 2), (1, 3)], 4)
-        multiply(later[:, 2 * block :], [(1, 4)], 6)
-        weave(last, 1, 0, 3, later[:], "gpsimd")
-        gather(small, 2)
-        activate([(1, 2), (1, 3)])
-        activate([(1, 4)])
-        store(1, 2, both)
-        final = held_b[:, 0, : 2 * C].bitcast(BF16)
-        multiply(later[:, :block], [(1, 5)], 4)
-        multiply(later[:, block:], [(1, 6), (1, 7)], 6)
-        weave(small, 1, 0, 2, final, "vector")
-        multiply(final[:, :block], [(1, 0)], 4)
-        activate([(1, 5)])
-        store(1, 5, both)
-        for h in range(2):
-            activate([(1, 6), (1, 7)], (h,))
-            store(1, 6, slice(h, h + 1))
-        multiply(final[:, block:], [(1, 1)], 6)
-        for e in range(2):
-            activate([(1, e)])
-            store(1, e, both)
+        def late(e):
+            gather(3, held0[e], e * C, U)
+
+        def weave(e0, count):
+            nc.vector.tensor_copy(
+                woven0[e0][:].bitcast(I32).rearrange("p (e n u) -> p e n u", e=count, u=2),
+                both0[e0 // 2][:, e0 % 2 : e0 % 2 + count].bitcast(I32).rearrange("p e u n -> p e n u"),
+            )
+
+        def close(e0, count):
+            quantise(woven0[e0][:], 0, e0)
+            for e in range(e0, e0 + count):
+                finish(0, (e,), 1 + e % 3)
+
+        late(0)
+        late(1)
+        late(2)
+        weave(0, 2)
+        late(3)
+        close(0, 2)
+        late(4)
+        weave(2, 2)
+        late(5)
+        close(2, 2)
+        weave(4, 1)
+        late(6)
+        close(4, 1)
+        weave(5, 1)
+        late(7)
+        close(5, 1)
+        weave(6, 1)
+        weave(7, 1)
+        close(6, 1)
+        close(7, 1)

@@ -22,12 +22,12 @@ FP4X4 = mybir.dt.float4_e2m1fn_x4
 ACT = mybir.ActivationFunctionType
 
 GROUP = 16
-EARLY = 2
+EARLY = 4
 TABLES = (
-    (1, 0, True, ((1280, 856, 0), (768, 512, 0))),
+    (1, 0, False, ((1280, 856, 0), (768, 512, 0))),
     (1, 1, False, ((1024, 0, 0), (1024, 680, 0))),
     (0, 0, False, ((1024, 0, 0), (1024, 0, 0))),
-    (0, 1, False, ((960, 0, 400), (704, 0, 288), (384, 0, 160))),
+    (0, 1, False, ((960, 0, 400), (704, 0, 288), (384, 256, 0))),
 )
 
 
@@ -46,7 +46,9 @@ def tile_moe_eps_lin_gelu_kernel(tc, xT, w_words, w_scales, b, offs, out):
         nc.scalar.activation(warm_out[:], warm_in[:], ACT.Gelu_apprx_tanh)
 
         w_codes = {}
+
         w_planes = {}
+        bias = keep.tile([P, 2, E], F32, name="bias")
 
         def load_scales(e0, count):
             plane = keep.tile([P, count * N], U8, name="plane%d" % e0, align_bytes=256)
@@ -59,13 +61,13 @@ def tile_moe_eps_lin_gelu_kernel(tc, xT, w_words, w_scales, b, offs, out):
             for k in range(count):
                 w_planes[e0 + k] = plane[:, k * N : (k + 1) * N]
 
-        def load_words(e0):
-            words = keep.tile([P, 2, 2 * N], U8, name="words%d" % e0, align_bytes=512)
+        def load_words(e0, count):
+            words = keep.tile([P, count, 2 * N], U8, name="words%d" % e0, align_bytes=512)
             nc.sync.dma_start(
                 out=words[:].bitcast(I32),
-                in_=w_words[e0 : e0 + 2].rearrange("e a p c -> p (e a) c").bitcast(I32),
+                in_=w_words[e0 : e0 + count].rearrange("e a p c -> p (e a) c").bitcast(I32),
             )
-            for k in range(2):
+            for k in range(count):
                 w_codes[e0 + k] = words[:, k, :]
 
         raws = []
@@ -77,8 +79,6 @@ def tile_moe_eps_lin_gelu_kernel(tc, xT, w_words, w_scales, b, offs, out):
             if whole:
                 raw = keep.tile([P, 2 * HALF], F32, name="raw%d" % i, align_bytes=1024)
                 nc.sync.dma_start(out=raw[:, :HALF], in_=source[:, 0, :])
-            if i == 0:
-                nc.sync.dma_start(offsets[:], offs)
             t0 = 0
             for n, v, g in cuts:
                 if whole:
@@ -88,20 +88,19 @@ def tile_moe_eps_lin_gelu_kernel(tc, xT, w_words, w_scales, b, offs, out):
                     piece = keep.tile([P, 2, n], F32, name="raw%d_%d" % (i, t0), align_bytes=1024)
                     nc.sync.dma_start(out=piece[:], in_=source[:, :, t0 : t0 + n])
                     pieces.append(piece[:])
+                if i == 0 and t0 == 0:
+                    nc.sync.dma_start(offsets[:], offs)
                 t0 = t0 + n
             raws.append(pieces)
 
-        bias = keep.tile([P, 2, E], F32, name="bias")
         for i in range(3):
             load_rows(i)
-        load_scales(0, EARLY)
+        load_scales(0, E)
         nc.sync.dma_start(out=bias[:], in_=b.rearrange("(h p) e -> p h e", h=2))
-        for e0 in range(0, EARLY, 2):
-            load_words(e0)
+        load_words(0, EARLY)
         load_rows(3)
-        load_scales(EARLY, E - EARLY)
         for e0 in range(EARLY, E, 2):
-            load_words(e0)
+            load_words(e0, 2)
 
         tables = []
         for i in range(4):
@@ -129,12 +128,13 @@ def tile_moe_eps_lin_gelu_kernel(tc, xT, w_words, w_scales, b, offs, out):
                 t0 = t0 + n
 
         held1 = [keep.tile([P, 2, 3 * U], U32, name="held1_%d" % g, align_bytes=256) for g in range(E // 2)]
-        both0 = [keep.tile([P, 2, 2, U], U32, name="held0_%d" % g, align_bytes=256) for g in range(E // 2)]
-        held0 = [both0[e // 2][:, e % 2] for e in range(E)]
+        work = keep.tile([P, (3 * E + 4) * U], U32, name="work", align_bytes=256)
+        woven_at = [E + 4 + 2 * e for e in range(E)]
+        second_at = [E, E + 1, E + 2, E + 3, E, woven_at[0], woven_at[2], woven_at[4]]
 
         def gather(i, held, first, count):
             entries = offsets[:, first // GROUP : (first + count) // GROUP]
-            nc.vector.tensor_copy(held[:, TABLES[i][1], :], tables[i][:].indirect(entries))
+            nc.vector.tensor_copy(held, tables[i][:].indirect(entries))
 
         tokens = {}
 
@@ -183,11 +183,11 @@ def tile_moe_eps_lin_gelu_kernel(tc, xT, w_words, w_scales, b, offs, out):
 
         round_rows(0)
         for g in range(E // 2):
-            gather(0, held1[g], 2 * g * C + U, 3 * U)
+            gather(0, held1[g][:, 0, :], 2 * g * C + U, 3 * U)
         round_rows(1)
         woven1 = [keep.tile([P, 4 * PACK * U], BF16, name="woven1_%d" % a, align_bytes=256) for a in range(2)]
         for g in range(E // 2):
-            gather(1, held1[g], 2 * g * C + U, 3 * U)
+            gather(1, held1[g][:, 1, :], 2 * g * C + U, 3 * U)
             words = woven1[g // 2][:, g % 2 * 2 * PACK * U : (g % 2 + 1) * 2 * PACK * U].bitcast(U32)
             nc.gpsimd.tensor_copy(
                 words.rearrange("p (e n u) -> p e n u", e=2, u=2),
@@ -197,30 +197,28 @@ def tile_moe_eps_lin_gelu_kernel(tc, xT, w_words, w_scales, b, offs, out):
         round_rows(2)
         quantise(woven1[1][:], 1, 4)
         for e in range(E):
-            gather(2, held0[e], e * C, U)
-        finish(1, (0, 1), 0)
-        round_rows(3)
-        for g in range(1, E // 2):
+            gather(2, work[:, e * U : (e + 1) * U], e * C, U)
+        for g in range(EARLY // 2):
             finish(1, (2 * g, 2 * g + 1), g)
-
-        steps = ((0, 2), (2, 2), (4, 1), (5, 1), (6, 1), (7, 1))
-        woven0 = {}
-        for e0, count in steps:
-            woven0[e0] = keep.tile([P, count * PACK * U], BF16, name="woven0_%d" % e0, align_bytes=256)
+        round_rows(3)
+        for e in range(EARLY, E):
+            finish(1, (e,), 2 + e % 4)
 
         def late(e):
-            gather(3, held0[e], e * C, U)
+            gather(3, work[:, second_at[e] * U : (second_at[e] + 1) * U], e * C, U)
 
         def weave(e0, count):
-            nc.vector.tensor_copy(
-                woven0[e0][:].bitcast(I32).rearrange("p (e n u) -> p e n u", e=count, u=2),
-                both0[e0 // 2][:, e0 % 2 : e0 % 2 + count].bitcast(I32).rearrange("p e u n -> p e n u"),
-            )
+            view = work[:].bitcast(I32)
+            blocks = view.rearrange("p (b n) -> p b n", n=count * U)
+            first, second = e0 // count, second_at[e0] // count
+            values = view[:, woven_at[e0] * U : (woven_at[e0] + 2 * count) * U].rearrange("p (n u) -> p n u", u=2)
+            pairs = blocks[:, first : second + 1 : second - first].rearrange("p u n -> p n u")
+            nc.vector.tensor_copy(values, pairs)
 
         def close(e0, count):
-            quantise(woven0[e0][:], 0, e0)
+            quantise(work[:, woven_at[e0] * U : (woven_at[e0] + 2 * count) * U].bitcast(BF16), 0, e0)
             for e in range(e0, e0 + count):
-                finish(0, (e,), 1 + e % 3)
+                finish(0, (e,), 2 + e % 4)
 
         late(0)
         late(1)

@@ -27,7 +27,7 @@ TABLES = (
     (1, 0, False, ((1280, 856, 0), (768, 512, 0))),
     (1, 1, False, ((1024, 0, 0), (1024, 680, 0))),
     (0, 0, False, ((1024, 0, 0), (1024, 0, 0))),
-    (0, 1, False, ((960, 0, 400), (704, 0, 288), (384, 256, 0))),
+    (0, 1, False, ((960, 0, 320), (704, 0, 192), (384, 384, 0))),
 )
 
 
@@ -120,7 +120,8 @@ def tile_moe_eps_lin_gelu_kernel(tc, xT, w_words, w_scales, b, offs, out):
                 mid, late = v // 4, (n - g) // 4
                 if v > 0:
                     nc.vector.tensor_copy(out=part[:, :mid], in_=rows[:, :mid])
-                nc.scalar.activation(part[:, mid:late], rows[:, mid:late], ACT.Copy)
+                if late > mid:
+                    nc.scalar.activation(part[:, mid:late], rows[:, mid:late], ACT.Copy)
                 if g > 0:
                     nc.gpsimd.tensor_copy(
                         part[:, late:].rearrange("p c j i -> p c i j"), rows[:, late:].rearrange("p c j i -> p c i j")
@@ -150,7 +151,10 @@ def tile_moe_eps_lin_gelu_kernel(tc, xT, w_words, w_scales, b, offs, out):
         results = {}
         for rank in range(R):
             for e0, count in ((0, 2), (2, 2), (4, 2), (6, 2)) if rank == 1 else ((0, 2), (2, 2), (4, 2), (6, 1), (7, 1)):
-                result = keep.tile([P, 2, count * U], F32, name="result%d_%d" % (rank, e0), align_bytes=1024)
+                if (rank, e0) == (1, 2):
+                    result = raws[3][1][:, :, : count * U]
+                else:
+                    result = keep.tile([P, 2, count * U], F32, name="result%d_%d" % (rank, e0), align_bytes=1024)[:]
                 for k in range(count):
                     results[(rank, e0 + k)] = (result, k, e0)
 
@@ -179,7 +183,7 @@ def tile_moe_eps_lin_gelu_kernel(tc, xT, w_words, w_scales, b, offs, out):
                     )
                 if (k + 1) * U == result.shape[2]:
                     c0 = rank * (S // R) + e0 * U
-                    nc.sync.dma_start(out=out_rows[:, :, c0 : c0 + result.shape[2]], in_=result[:])
+                    nc.sync.dma_start(out=out_rows[:, :, c0 : c0 + result.shape[2]], in_=result)
 
         round_rows(0)
         for g in range(E // 2):
@@ -198,9 +202,9 @@ def tile_moe_eps_lin_gelu_kernel(tc, xT, w_words, w_scales, b, offs, out):
         quantise(woven1[1][:], 1, 4)
         for e in range(E):
             gather(2, work[:, e * U : (e + 1) * U], e * C, U)
-        for g in range(EARLY // 2):
-            finish(1, (2 * g, 2 * g + 1), g)
+        finish(1, (0, 1), 0)
         round_rows(3)
+        finish(1, (2, 3), 1)
         for e in range(EARLY, E):
             finish(1, (e,), 2 + e % 4)
 

@@ -24,9 +24,9 @@ ACT = mybir.ActivationFunctionType
 GROUP = 16
 EARLY = 4
 TABLES = (
-    (1, 0, False, ((1280, 856, 0), (768, 512, 0))),
-    (1, 1, False, ((1024, 0, 0), (1024, 680, 0))),
-    (0, 0, False, ((1024, 0, 0), (1024, 0, 0))),
+    (1, 0, False, ((2048, 1368, 0),)),
+    (1, 1, False, ((1152, 0, 0), (896, 512, 0))),
+    (0, 0, False, ((768, 0, 0), (768, 0, 0), (512, 0, 0))),
     (0, 1, False, ((960, 0, 320), (704, 0, 192), (384, 384, 0))),
 )
 
@@ -85,7 +85,8 @@ def tile_moe_eps_lin_gelu_kernel(tc, xT, w_words, w_scales, b, offs, out):
                     nc.sync.dma_start(out=raw[:, HALF + t0 : HALF + t0 + n], in_=source[:, 1, t0 : t0 + n])
                     pieces.append(raw[:].rearrange("p (j t) -> p j t", j=2)[:, :, t0 : t0 + n])
                 else:
-                    piece = keep.tile([P, 2, n], F32, name="raw%d_%d" % (i, t0), align_bytes=1024)
+                    name = "raw%d_%d" % (i, t0)
+                    piece = keep.tile([P, 2, n], F32, name=name, tag=name, align_bytes=1024)
                     nc.sync.dma_start(out=piece[:], in_=source[:, :, t0 : t0 + n])
                     pieces.append(piece[:])
                 if i == 0 and t0 == 0:
@@ -129,9 +130,9 @@ def tile_moe_eps_lin_gelu_kernel(tc, xT, w_words, w_scales, b, offs, out):
                 t0 = t0 + n
 
         held1 = [keep.tile([P, 2, 3 * U], U32, name="held1_%d" % g, align_bytes=256) for g in range(E // 2)]
-        work = keep.tile([P, (3 * E + 4) * U], U32, name="work", align_bytes=256)
-        woven_at = [E + 4 + 2 * e for e in range(E)]
-        second_at = [E, E + 1, E + 2, E + 3, E, woven_at[0], woven_at[2], woven_at[4]]
+        work = keep.tile([P, (3 * E + 6) * U], U32, name="work", align_bytes=256)
+        woven_at = [E + 6 + 2 * e for e in range(E)]
+        second_at = [E, E + 1, E + 2, E + 3, E + 4, E + 2, woven_at[2], woven_at[4]]
 
         def gather(i, held, first, count):
             entries = offsets[:, first // GROUP : (first + count) // GROUP]
@@ -139,9 +140,9 @@ def tile_moe_eps_lin_gelu_kernel(tc, xT, w_words, w_scales, b, offs, out):
 
         tokens = {}
 
-        def quantise(values, rank, e0):
+        def quantise(values, rank, e0, tag=""):
             n = values.shape[1] // PACK
-            codes = keep.tile([P, n], U32, name="codes%d_%d" % (rank, e0), align_bytes=256)
+            codes = keep.tile([P, n], U32, name="codes%d_%d" % (rank, e0), tag=tag, align_bytes=1024)
             scales = keep.tile([P, n], U8, name="scales%d_%d" % (rank, e0), align_bytes=256)
             nc.vector.quantize_mx(out=codes[:].bitcast(FP8X4), scales=scales[:], in_=values)
             for k in range(n // U):
@@ -153,6 +154,10 @@ def tile_moe_eps_lin_gelu_kernel(tc, xT, w_words, w_scales, b, offs, out):
             for e0, count in ((0, 2), (2, 2), (4, 2), (6, 2)) if rank == 1 else ((0, 2), (2, 2), (4, 2), (6, 1), (7, 1)):
                 if (rank, e0) == (1, 2):
                     result = raws[3][1][:, :, : count * U]
+                elif (rank, e0) == (1, 4):
+                    result = work[:].bitcast(F32).rearrange("p (b n) -> p b n", n=2 * U)[:, 0 : E // 2 + 1 : E // 2]
+                elif (rank, e0) == (1, 6):
+                    result = work[:, woven_at[0] * U : woven_at[2] * U].bitcast(F32).rearrange("p (h n) -> p h n", h=2)
                 else:
                     result = keep.tile([P, 2, count * U], F32, name="result%d_%d" % (rank, e0), align_bytes=1024)[:]
                 for k in range(count):
@@ -199,41 +204,46 @@ def tile_moe_eps_lin_gelu_kernel(tc, xT, w_words, w_scales, b, offs, out):
             )
         quantise(woven1[0][:], 1, 0)
         round_rows(2)
-        quantise(woven1[1][:], 1, 4)
         for e in range(E):
             gather(2, work[:, e * U : (e + 1) * U], e * C, U)
+            if e == 1:
+                quantise(woven1[1][:], 1, 4, "raw2_1536")
         finish(1, (0, 1), 0)
         round_rows(3)
         finish(1, (2, 3), 1)
-        for e in range(EARLY, E):
-            finish(1, (e,), 2 + e % 4)
 
         def late(e):
             gather(3, work[:, second_at[e] * U : (second_at[e] + 1) * U], e * C, U)
 
         def weave(e0, count):
-            view = work[:].bitcast(I32)
+            view = work[:] if e0 == 0 else work[:].bitcast(I32)
             blocks = view.rearrange("p (b n) -> p b n", n=count * U)
             first, second = e0 // count, second_at[e0] // count
             values = view[:, woven_at[e0] * U : (woven_at[e0] + 2 * count) * U].rearrange("p (n u) -> p n u", u=2)
             pairs = blocks[:, first : second + 1 : second - first].rearrange("p u n -> p n u")
-            nc.vector.tensor_copy(values, pairs)
+            if e0 == 0:
+                nc.scalar.copy(values, pairs)
+            else:
+                nc.vector.tensor_copy(values, pairs)
 
         def close(e0, count):
             quantise(work[:, woven_at[e0] * U : (woven_at[e0] + 2 * count) * U].bitcast(BF16), 0, e0)
+            if e0 == 0:
+                for e in range(EARLY, E):
+                    finish(1, (e,), 2 + e % 4)
             for e in range(e0, e0 + count):
                 finish(0, (e,), 2 + e % 4)
 
         late(0)
         late(1)
-        late(2)
         weave(0, 2)
+        late(2)
         late(3)
         close(0, 2)
-        late(4)
         weave(2, 2)
-        late(5)
+        late(4)
         close(2, 2)
+        late(5)
         weave(4, 1)
         late(6)
         close(4, 1)

@@ -24,10 +24,10 @@ ACT = mybir.ActivationFunctionType
 GROUP = 16
 EARLY = 4
 TABLES = (
-    (1, 0, False, ((2048, 1368, 0),)),
-    (1, 1, False, ((1152, 0, 0), (896, 512, 0))),
+    (1, 0, False, ((1280, 856, 0), (768, 512, 0))),
+    (1, 1, False, ((1024, 0, 0), (1024, 640, 0))),
     (0, 0, False, ((768, 0, 0), (768, 0, 0), (512, 0, 0))),
-    (0, 1, False, ((960, 0, 320), (704, 0, 192), (384, 384, 0))),
+    (0, 1, False, ((960, 0, 352), (704, 0, 224), (384, 288, 0))),
 )
 
 
@@ -153,7 +153,7 @@ def tile_moe_eps_lin_gelu_kernel(tc, xT, w_words, w_scales, b, offs, out):
         for rank in range(R):
             for e0, count in ((0, 2), (2, 2), (4, 2), (6, 2)) if rank == 1 else ((0, 2), (2, 2), (4, 2), (6, 1), (7, 1)):
                 if (rank, e0) == (1, 2):
-                    result = raws[3][1][:, :, : count * U]
+                    result = raws[3][2][:, :, U:]
                 elif (rank, e0) == (1, 4):
                     result = work[:].bitcast(F32).rearrange("p (b n) -> p b n", n=2 * U)[:, 0 : E // 2 + 1 : E // 2]
                 elif (rank, e0) == (1, 6):

from contextlib import ExitStack

import concourse.mybir as mybir

K, T, E, C, N = 512, 4096, 8, 256, 256
R = 2
P = 128
PACK = 4
S = E * C
U = C // R
HALF = T // R
FLOPS = 2 * K * N * S

F32 = mybir.dt.float32
BF16 = mybir.dt.bfloat16
U32 = mybir.dt.uint32
I32 = mybir.dt.int32
U16 = mybir.dt.uint16
U8 = mybir.dt.uint8
FP8X4 = mybir.dt.float8_e4m3fn_x4
FP4X4 = mybir.dt.float4_e2m1fn_x4
ACT = mybir.ActivationFunctionType

GROUP = 16
EARLY = 4
TABLES = (
    (1, 0, False, ((1280, 856, 0), (768, 512, 0))),
    (1, 1, False, ((1024, 0, 0), (1024, 640, 0))),
    (0, 0, False, ((768, 0, 0), (768, 0, 0), (512, 0, 0))),
    (0, 1, False, ((960, 0, 352), (704, 0, 224), (384, 288, 0))),
)


def tile_moe_eps_lin_gelu_kernel(tc, xT, w_words, w_scales, b, offs, out):
    nc = tc.nc
    with ExitStack() as ctx:
        keep = ctx.enter_context(tc.tile_pool(name="keep", bufs=1))
        psum = ctx.enter_context(tc.psum_pool(name="psum", bufs=1))

        offsets = keep.tile([P, S // GROUP], U16, name="offsets")
        x_rows = xT.rearrange("(p j) t -> p j t", j=PACK)

        warm_in = keep.tile([P, 1], F32, name="warm_in")
        warm_out = keep.tile([P, 1], F32, name="warm_out")
        nc.gpsimd.memset(warm_in[:], 0.0)
        nc.scalar.activation(warm_out[:], warm_in[:], ACT.Gelu_apprx_tanh)

        w_codes = {}

        w_planes = {}
        bias = keep.tile([P, 2, E], F32, name="bias")

        def load_scales(e0, count):
            plane = keep.tile([P, count * N], U8, name="plane%d" % e0, align_bytes=256)
            nc.gpsimd.memset(plane[:].bitcast(I32), 0)
            for q in range(4):
                nc.sync.dma_start(
                    out=plane[q:P:32, :].rearrange("q (e n) -> q e n", e=count).bitcast(I32),
                    in_=w_scales[e0 : e0 + count, 0, q:16:4, :].rearrange("e q n -> q e n").bitcast(I32),
                )
            for k in range(count):
                w_planes[e0 + k] = plane[:, k * N : (k + 1) * N]

        def load_words(e0, count):
            words = keep.tile([P, count, 2 * N], U8, name="words%d" % e0, align_bytes=512)
            nc.sync.dma_start(
                out=words[:].bitcast(I32),
                in_=w_words[e0 : e0 + count].rearrange("e a p c -> p (e a) c").bitcast(I32),
            )
            for k in range(count):
                w_codes[e0 + k] = words[:, k, :]

        raws = []

        def load_rows(i):
            rank, pair, whole, cuts = TABLES[i]
            source = x_rows[:, 2 * pair : 2 * pair + 2, rank * HALF : (rank + 1) * HALF]
            pieces = []
            if whole:
                raw = keep.tile([P, 2 * HALF], F32, name="raw%d" % i, align_bytes=1024)
                nc.sync.dma_start(out=raw[:, :HALF], in_=source[:, 0, :])
            t0 = 0
            for n, v, g in cuts:
                if whole:
                    nc.sync.dma_start(out=raw[:, HALF + t0 : HALF + t0 + n], in_=source[:, 1, t0 : t0 + n])
                    pieces.append(raw[:].rearrange("p (j t) -> p j t", j=2)[:, :, t0 : t0 + n])
                else:
                    name = "raw%d_%d" % (i, t0)
                    piece = keep.tile([P, 2, n], F32, name=name, tag=name, align_bytes=1024)
                    nc.sync.dma_start(out=piece[:], in_=source[:, :, t0 : t0 + n])
                    pieces.append(piece[:])
                if i == 0 and t0 == 0:
                    nc.sync.dma_start(offsets[:], offs)
                t0 = t0 + n
            raws.append(pieces)

        for i in range(3):
            load_rows(i)
        load_scales(0, E)
        nc.sync.dma_start(out=bias[:], in_=b.rearrange("(h p) e -> p h e", h=2))
        load_words(0, EARLY)
        load_rows(3)
        for e0 in range(EARLY, E, 2):
            load_words(e0, 2)

        tables = []
        for i in range(4):
            rank = TABLES[i][0]
            table = keep.tile([P, (rank + 1) * HALF], U32, name="table%d" % i, align_bytes=256)
            if rank == 1:
                nc.vector.memset(table[:, :HALF].bitcast(I32), 0)
            tables.append(table)

        def round_rows(i):
            rank, pair, whole, cuts = TABLES[i]
            pairs = tables[i][:, rank * HALF :].bitcast(BF16).rearrange("p (c i j) -> p c j i", i=4, j=2)
            t0 = 0
            for (n, v, g), piece in zip(cuts, raws[i]):
                rows = piece.rearrange("p j (c i) -> p c j i", i=4)
                part = pairs[:, t0 // 4 : (t0 + n) // 4]
                mid, late = v // 4, (n - g) // 4
                if v > 0:
                    nc.vector.tensor_copy(out=part[:, :mid], in_=rows[:, :mid])
                if late > mid:
                    nc.scalar.activation(part[:, mid:late], rows[:, mid:late], ACT.Copy)
                if g > 0:
                    nc.gpsimd.tensor_copy(
                        part[:, late:].rearrange("p c j i -> p c i j"), rows[:, late:].rearrange("p c j i -> p c i j")
                    )
                t0 = t0 + n

        held1 = [keep.tile([P, 2, 3 * U], U32, name="held1_%d" % g, align_bytes=256) for g in range(E // 2)]
        work = keep.tile([P, (3 * E + 6) * U], U32, name="work", align_bytes=256)
        woven_at = [E + 6 + 2 * e for e in range(E)]
        second_at = [E, E + 1, E + 2, E + 3, E + 4, E + 2, woven_at[2], woven_at[4]]

        def gather(i, held, first, count):
            entries = offsets[:, first // GROUP : (first + count) // GROUP]
            nc.vector.tensor_copy(held, tables[i][:].indirect(entries))

        tokens = {}

        def quantise(values, rank, e0, tag=""):
            n = values.shape[1] // PACK
            codes = keep.tile([P, n], U32, name="codes%d_%d" % (rank, e0), tag=tag, align_bytes=1024)
            scales = keep.tile([P, n], U8, name="scales%d_%d" % (rank, e0), align_bytes=256)
            nc.vector.quantize_mx(out=codes[:].bitcast(FP8X4), scales=scales[:], in_=values)
            for k in range(n // U):
                tokens[(rank, e0 + k)] = (codes[:, k * U : (k + 1) * U], scales[:, k * U : (k + 1) * U])

        out_rows = out.rearrange("(h p) c -> p h c", h=2)
        results = {}
        for rank in range(R):
            for e0, count in ((0, 2), (2, 2), (4, 2), (6, 2)) if rank == 1 else ((0, 2), (2, 2), (4, 2), (6, 1), (7, 1)):
                if (rank, e0) == (1, 2):
                    result = raws[3][2][:, :, U:]
                elif (rank, e0) == (1, 4):
                    result = work[:].bitcast(F32).rearrange("p (b n) -> p b n", n=2 * U)[:, 0 : E // 2 + 1 : E // 2]
                elif (rank, e0) == (1, 6):
                    result = work[:, woven_at[0] * U : woven_at[2] * U].bitcast(F32).rearrange("p (h n) -> p h n", h=2)
                else:
                    result = keep.tile([P, 2, count * U], F32, name="result%d_%d" % (rank, e0), align_bytes=1024)[:]
                for k in range(count):
                    results[(rank, e0 + k)] = (result, k, e0)

        def finish(rank, experts, bank_number):
            bank = psum.tile([P, len(experts), 2, U], F32, name="bank%d" % bank_number)
            for i, e in enumerate(experts):
                codes, scales = tokens[(rank, e)]
                for h in range(2):
                    nc.tensor.matmul_mx(
                        out=bank[:, i, h, :],
                        lhsT=w_codes[e][:, 256 * h : 256 * h + 256].bitcast(FP4X4),
                        lhsT_scale=w_planes[e][:, 128 * h : 128 * h + 128],
                        rhs=codes.bitcast(FP8X4),
                        rhs_scale=scales,
                        start=True,
                        stop=True,
                    )
            for i, e in enumerate(experts):
                result, k, e0 = results[(rank, e)]
                for h in range(2):
                    nc.scalar.activation(
                        result[:, h, k * U : (k + 1) * U],
                        bank[:, i, h, :],
                        ACT.Gelu_apprx_tanh,
                        bias=bias[:, h, e : e + 1],
                    )
                if (k + 1) * U == result.shape[2]:
                    c0 = rank * (S // R) + e0 * U
                    nc.sync.dma_start(out=out_rows[:, :, c0 : c0 + result.shape[2]], in_=result)

        round_rows(0)
        for g in range(E // 2):
            gather(0, held1[g][:, 0, :], 2 * g * C + U, 3 * U)
        round_rows(1)
        woven1 = [keep.tile([P, 4 * PACK * U], BF16, name="woven1_%d" % a, align_bytes=256) for a in range(2)]
        for g in range(E // 2):
            gather(1, held1[g][:, 1, :], 2 * g * C + U, 3 * U)
            words = woven1[g // 2][:, g % 2 * 2 * PACK * U : (g % 2 + 1) * 2 * PACK * U].bitcast(U32)
            nc.gpsimd.tensor_copy(
                words.rearrange("p (e n u) -> p e n u", e=2, u=2),
                held1[g][:].rearrange("p u (b n) -> p b n u", n=U)[:, 0:3:2],
            )
        quantise(woven1[0][:], 1, 0)
        round_rows(2)
        for e in range(E):
            gather(2, work[:, e * U : (e + 1) * U], e * C, U)
            if e == 1:
                quantise(woven1[1][:], 1, 4, "raw2_1536")
        finish(1, (0, 1), 0)
        round_rows(3)
        finish(1, (2, 3), 1)

        def late(e):
            gather(3, work[:, second_at[e] * U : (second_at[e] + 1) * U], e * C, U)

        def weave(e0, count):
            view = work[:] if e0 == 0 else work[:].bitcast(I32)
            blocks = view.rearrange("p (b n) -> p b n", n=count * U)
            first, second = e0 // count, second_at[e0] // count
            values = view[:, woven_at[e0] * U : (woven_at[e0] + 2 * count) * U].rearrange("p (n u) -> p n u", u=2)
            pairs = blocks[:, first : second + 1 : second - first].rearrange("p u n -> p n u")
            if e0 == 0:
                nc.scalar.copy(values, pairs)
            else:
                nc.vector.tensor_copy(values, pairs)

        def close(e0, count):
            quantise(work[:, woven_at[e0] * U : (woven_at[e0] + 2 * count) * U].bitcast(BF16), 0, e0)
            if e0 == 0:
                for e in range(EARLY, E):
                    finish(1, (e,), 2 + e % 4)
            for e in range(e0, e0 + count):
                finish(0, (e,), 2 + e % 4)

        late(0)
        late(1)
        weave(0, 2)
        late(2)
        late(3)
        close(0, 2)
        weave(2, 2)
        late(4)
        close(2, 2)
        late(5)
        weave(4, 1)
        late(6)
        close(4, 1)
        weave(5, 1)
        late(7)
        close(5, 1)
        weave(6, 1)
        weave(7, 1)
        close(6, 1)
        close(7, 1)
